import numpy as np, ml_dtypes
CORES = [2,6,10,14,18,22,26,30]
N = 8
import mx_ref
BF = ml_dtypes.bfloat16
def gentries(a):
    return np.ascontiguousarray(a.reshape(8, 16, -1).transpose(0, 2, 1)).reshape(8, -1)
def gtable(e):
    e = np.asarray(e); return np.ascontiguousarray(e.reshape(8, -1, 16).transpose(0, 2, 1)).reshape(128, -1).astype(np.int32)
def gcols(t, e):
    v = np.concatenate([t.reshape(8, 16, -1, 4), np.zeros((8, 16, 1, 4), BF)], axis=2)
    return np.ascontiguousarray(np.stack([v[g][:, e[g]] for g in range(8)])).reshape(128, -1)
def tile(rs):
    return np.stack(rs, axis=2).reshape(128, -1).astype(BF)
def pick(q, e):
    c = np.concatenate([q[0].reshape(128, -1, 4), np.zeros((128, 1, 4), np.uint8)], axis=1); s = np.concatenate([q[1], np.ones((16, 1), np.uint8)], axis=1)
    return (np.ascontiguousarray(c[:, e].reshape(128, -1)), np.ascontiguousarray(s[:, e]))
def join(*qs):
    return (np.concatenate([q[0] for q in qs], axis=1), np.concatenate([q[1] for q in qs], axis=1))
def put(q, e, v):
    c, s = q[0].reshape(128, -1, 4).copy(), q[1].copy(); c[:, e] = v[0].reshape(128, -1, 4); s[:, e] = v[1]
    return (c.reshape(128, -1), s)
def pk(c, s):
    return (np.ascontiguousarray(c), mx_ref.live(s))
def emit(q):
    return q[0], q[1]
def packed(v, rng):
    q = [mx_ref.quantize(np.ascontiguousarray(v[r])) for r in range(N)]
    return np.stack([a for a, b in q]), np.stack([mx_ref.plane(b, rng) for a, b in q])
def values_of_codes():
    e, c = np.zeros((128, 128, 4), np.float32), np.zeros((128, 2, 4), np.uint8)
    e[np.arange(128), np.arange(128), 0] = 1
    c[:127, :, 0] = np.arange(256).reshape(2, 128).T[:127]
    return mx_ref.matmul(mx_ref.quantize(e.reshape(128, 512).astype(BF)), (c.reshape(128, 8), np.full((16, 2), 127, np.uint8))).T.reshape(-1).astype(np.float64)
CODE_VALUE, SCALE_VALUE = values_of_codes(), 2.0 ** (np.arange(256) - 127.0)
def decode(q):
    return (CODE_VALUE[q[0]].reshape(16, 8, -1, 4) * SCALE_VALUE[q[1]][:, None, :, None] + 0.0).reshape(128, -1).astype(np.float32)
def f(rng, *shape):
    return mx_ref.flush((rng.standard_normal(shape, dtype=np.float32) * np.exp2(rng.integers(-2, 3, shape[:-1] + (1,)))).astype(BF))
def wide(rng, *shape, cols=0):
    v = rng.standard_normal(shape, dtype=np.float32) * np.exp2(rng.integers(-12, 13, shape)).astype(np.float32)
    if cols: v *= np.repeat(np.exp2(rng.integers(-cols, cols + 1, shape[:-2] + (1, shape[-1] // 4))) * (rng.random(shape[:-2] + (1, shape[-1] // 4)) > 0.0625), 4, axis=-1).astype(np.float32)
    return mx_ref.flush(v.astype(BF))
C, M = 256, 8
STEP = [1, 2, 4]
BASE = np.arange(C) // 32 * 32
def big(v):
    v = v.astype(np.float32)
    v[np.abs(v) < np.float32(2.0 ** -16)] = 0
    return v.astype(BF)
def numbers_of(rng):
    return {"x": big(f(rng, N, 128, 4 * C)), "u": np.array(f(rng, N, 128, 512)), "v": np.array(f(rng, N, 128, 512))}
def functions(e):
    return np.stack([gtable(e[r] + BASE) for r in range(N)])
def layers(rng, still=[]):
    w = big(f(rng, N, 128, 2048)).reshape(N, 8, 16, 4, 8, 16, 4)
    for i in still:
        w[:, :, i] = 0
        w[:, :, :, :, :, i] = 0
    return w
def weights(rng, w):
    c, p = packed(np.ascontiguousarray(w).reshape(N, 128, 2048), rng)
    return {"wc": c, "ws": p}
def setup_inputs(rng):
    return {**numbers_of(rng), "fn": functions(rng.integers(0, 32, (N, 8, C))), **weights(rng, layers(rng))}
def setup_inputs_ties(rng):
    d = numbers_of(rng)
    x = d["x"].reshape(N, 8, 16, C, 4)
    even = np.repeat(rng.permutation(C // 32) % 2 == 0, 32)
    k = np.where(even, np.repeat(rng.integers(1, 3, (1, 8, C // 32)), 32, axis=2), rng.integers(0, 3, (N, 8, C)))
    e = rng.integers(0, 32, (N, 8, C))
    e = np.where(even, e[:1], e)
    x[:, :, 0] = 0
    x[:, :, 0, :, 0] = k.astype(np.float32).astype(BF)
    u = d["u"].reshape(N, 128, 128, 4)
    u[:, :, ::16] = 0
    o = rng.permutation(N)
    for r in range(N):
        for h in range(0, 128, 16): u[r, h, h, 0] = 0.0 if r == o[0] else -1.0 if r == o[1] else 1.0
    return {"x": x.reshape(N, 128, 4 * C), "u": u.reshape(N, 128, 512), "v": d["v"], "fn": functions(e), **weights(rng, layers(rng, [0]))}
def setup_inputs_near(rng):
    d = numbers_of(rng)
    x = d["x"].astype(np.float32).reshape(N, 8, 16, C, 4)
    x[:, :, 0] = 0
    x[:, :, 8:] = 0
    far = np.repeat(rng.permutation(C // 32) % 2 == 0, 32)
    c = np.repeat(rng.integers(0, 2, (1, 8, C // 32)) * 2.0 - 1.0, 32, axis=2)
    s = rng.integers(0, 16, (N, 8, C))
    x[:, :, 0, :, 0] = np.where(far, 0.0, c)
    x[:, :, 11, :, 0] = np.where(far, 0.0, 2.0 ** -10)
    x[:, :, 8] = np.where(far[:, None], rng.integers(-1, 2, (N, 8, C, 4)) * 2.0 ** -22, ((s[:, :, :, None] >> np.arange(4)) & 1) * np.exp2(np.arange(4) - 23.0))
    u = d["u"].reshape(N, 128, 128, 4)
    u[:, :, ::16] = 0
    o = rng.permutation(N) % 2
    for r in range(N):
        k = 1.0 if o[r] == 0 else 2.0 ** -30
        for h in range(0, 128, 16):
            u[r, h, h, 0] = k
            u[r, h + 8, h] = k
            u[r, h + 11, h, 0] = k
    return {"x": x.reshape(N, 128, 4 * C).astype(BF), "u": u.reshape(N, 128, 512), "v": d["v"], "fn": functions(rng.integers(0, 32, (N, 8, C))), **weights(rng, layers(rng, [0, 8, 9, 10, 11, 12, 13, 14, 15]))}
def setup_inputs_huge(rng):
    d = numbers_of(rng)
    o = rng.permutation(N)
    k = np.repeat(rng.permutation(C // 32) % 3, 32)
    c = np.where(k == 2, rng.choice([-1.0, 1.0], (N, C)), k * 2.0 - 1.0)
    x = 2.0 ** 30 * (0.6 + 0.4 * rng.random((N, 8, 1, C, 1))) * (1.0 - 0.02 * rng.random((N, 8, 16, C, 4))) * c[:, None, None, :, None]
    a = 2.0 ** 29 * (1.0 - 0.1 * rng.random((N, 8, 16, 8, 4)))
    for g in range(8): a[:, g, :, g] *= 2.0
    for r in range(N):
        if o[r] == 0: a[r] = 2.0 ** 30
        if o[r] % 2 == 1: a[r] *= -1.0
    u = d["u"].reshape(N, 128, 128, 4)
    u[:, :, ::16] = a.reshape(N, 128, 8, 4).astype(np.float32).astype(BF)
    w = np.zeros((N, 128, 4, 128, 4), np.float32)
    i = np.arange(128)
    for b in range(4): w[:, i, b, i, b] = -1
    return {"x": x.astype(np.float32).reshape(N, 128, 4 * C).astype(BF), "u": u.reshape(N, 128, 512), "v": d["v"], "fn": functions(rng.integers(0, 32, (N, 8, C))), **weights(rng, w.astype(BF))}
def setup_inputs_paths(rng):
    d = numbers_of(rng)
    x = d["x"].astype(np.float32).reshape(N, 8, 16, C, 4)
    e, top = np.zeros((N, 8, C // 32, 32), np.int64), np.zeros((N, 8, C // 32), np.int64)
    size = [1, M - 1, M, M + 1, 24, 32]
    o = rng.permutation(8)
    for r in range(N):
        for g in range(8):
            for b in range(C // 32):
                k, a = int(o[r] + g + b) % 8, rng.permutation(32)
                top[r, g, b] = a[0]
                e[r, g, b] = a
                if k == 7: top[r, g, b] = rng.integers(32)
                if k < 6:
                    n = size[k]
                    e[r, g, b] = a[rng.integers(0, n, 32)]
                    e[r, g, b, a[:n]] = np.append(a[1:n], a[n - 1])
    s = rng.integers(0, 3, (N, 8, C // 32, 32)) * 0.5
    np.put_along_axis(s, top[:, :, :, None], 1.5, axis=3)
    x[:, :, 0] = 0
    x[:, :, 0, :, 0] = s.reshape(N, 8, C)
    z = np.exp2(rng.integers(-13, -6, (N, 8, 8, 1, 4)) * 1.0) * (1.0 + (2 * rng.integers(0, 64, (N, 8, 8, 1, 4)) + 1) * 2.0 ** -7) * rng.choice([-1.0, 1.0], (N, 8, 8, 1, 4))
    z[:, :, 0, :, 0] = 1.96875
    x[:, :, 8:] = z
    u = d["u"].reshape(N, 128, 128, 4)
    u[:, :, ::16] = 0
    for h in range(0, 128, 16): u[:, h, h, 0] = 1
    return {"x": x.reshape(N, 128, 4 * C).astype(BF), "u": u.reshape(N, 128, 512), "v": d["v"], "fn": functions(e.reshape(N, 8, C)), **weights(rng, layers(rng, [0, 8, 9, 10, 11, 12, 13, 14, 15]))}
def setup_inputs_spread(rng):
    d = setup_inputs(rng)
    d["x"] = big(wide(rng, N, 128, 4 * C, cols=6))
    return d
def check_inputs(d):
    b = []
    for k in ("x", "u", "v"):
        a = np.abs(d[k].astype(np.float32))
        if not (np.isfinite(a).all() and ((a == 0) | (a >= 2.0 ** -30) & (a <= 2.0 ** 30)).all()): b.append("a value of " + k)
    none, least, most = [emit(mx_ref.quantize(np.full((128, 16), k, np.float32).astype(BF)))[1][0, 0] for k in (0.0, 2.0 ** -30, 2.0 ** 30)]
    for r in range(N):
        if (gentries(d["fn"][r]) // 32 * 32 != BASE).any(): b.append("fn: an entry out of its block")
        if ((d["wc"][r] == 0x7F) | (d["wc"][r] == 0xFF)).any(): b.append("wc: a code that is no number")
        s = mx_ref.live(d["ws"][r])
        if ((s != none) & ((s < least) | (s > most))).any(): b.append("ws: a scale out of range")
    return b
def reread(fun, head):
    row = np.arange(len(fun))
    a = fun
    for k in range(5): a = np.take_along_axis(a, a, axis=1)
    cyc = np.zeros(fun.shape, bool)
    np.put_along_axis(cyc, a, True, axis=1)
    many = np.count_nonzero(cyc, axis=1)
    w = np.take_along_axis(fun, np.argsort(~cyc, axis=1, kind="stable"), axis=1)
    up = fun.copy()
    for j in range(31):
        i = row[j + 1 < many]
        up[i, w[i, j]] = w[i, j + 1]
    root = w[row, many - 1]
    path, at, on = np.full(fun.shape, -1), head, np.ones(len(fun), bool)
    for j in range(32):
        path[:, j] = np.where(on, at, -1)
        on = on & (at != root)
        at = up[row, at]
    q = np.sort(np.where(path < 0, 32, path), axis=1)
    for j in range(32):
        i = row[path[:, j] >= 0]
        up[i, q[i, j]] = path[i, j]
    return up, path
def reference(x, u, v, fn, wc, ws):
    qu = [mx_ref.quantize(u[r]) for r in range(N)]
    lay = [pk(wc[r], ws[r]) for r in range(N)]
    now = [x[r] for r in range(N)]
    fun = np.stack([gentries(fn[r]) - BASE for r in range(N)]).astype(np.int64).reshape(-1, 32)
    row = np.arange(len(fun))
    block = row % (C // 32)
    for t in STEP:
        s = np.stack([mx_ref.matmul(qu[r], mx_ref.quantize(now[r]))[::16] + np.float32(0.0) for r in range(N)])
        fun, path = reread(fun, np.argmax(s.reshape(-1, 32), axis=1))
        to = fun.reshape(N, 8, C) + BASE
        give = np.where(path < 0, -1, path + 32 * block[:, None])[:, :M].reshape(N, 8, -1)
        take = np.full(path.shape, -1)
        for j in range(M):
            i = row[path[:, j] >= 0]
            take[i, path[i, j]] = M * block[i] + j
        take = take.reshape(N, 8, C)
        made, sent = [], []
        for r in range(N):
            z = ((now[r].astype(np.float32) + gcols(now[r], to[r]).astype(np.float32)) * np.float32(0.5)).astype(BF)
            q = mx_ref.quantize(z)
            made.append(tile([mx_ref.matmul(pick(lay[r], np.arange(128 * b, 128 * b + 128)), q) * np.float32(0.03125) + z[:, b::4].astype(np.float32) for b in range(4)]))
            sent.append(mx_ref.quantize(gcols(made[r], give[r])))
        for r in range(N):
            came = gcols(decode(sent[r ^ t]).astype(BF), take[r]).astype(np.float32)
            half = ((made[r].astype(np.float32) + came) * np.float32(0.5)).astype(BF)
            now[r] = np.where(np.repeat(np.repeat(take[r] >= 0, 16, axis=0), 4, axis=1), half, made[r])
    y, fo = np.zeros((N, 128, C), np.float32), np.zeros((N, 8, C), np.float32)
    oc, osc = np.zeros((N, 128, 4 * C), np.uint8), np.zeros((N, 16, C), np.uint8)
    for r in range(N):
        q = mx_ref.quantize(now[r])
        y[r] = mx_ref.matmul(mx_ref.quantize(v[r]), q)
        fo[r] = to[r]
        oc[r], osc[r] = emit(q)
    return {"y": y, "fo": fo, "oc": oc, "osc": osc}

@@ -1,0 +1,496 @@
+from concourse.mybir import dt, AluOpType, ActivationFunctionType
+
+A = AluOpType
+AF = ActivationFunctionType
+F32, BF, I32, U16, Q8, U8 = "float32", "bfloat16", "int32", "uint16", "float8_e4m3fn_x4", "uint8"
+SIZE = {F32: 4, BF: 2, I32: 4, U16: 2, Q8: 4, U8: 1}
+STEP = [1, 2, 4]
+RW = 144
+BIGC = 1.0e29
+
+SCRATCH = {}
+for _t, _l in [
+    (I32, "fni16 pI16 rI16 vb256 tb512"),
+    (U16, "cl48 fl80 ul80 ol16 dl16 ho_4 ls_32 lp_16 zl_32"),
+    (BF, "ut512 vt512 et516 smb96 cs128 cq128 tw128 tx256 ty256 seg128 ci128 rf256 ra256 rb256 ex256 smx256 smn256 nc256 uo1024 ub1728 "
+         "x_640 xh_512 xg_512 z_512 zz_512 y_640 p_512 ph_128 pn_128 nf_128 sh_128 fw_256 fr_128 ez_128"),
+    (F32, "col32 bi224 bt224 jj40 kx16 sm160 tab24 kd16 kk24 cm128 jb128 hc8 dd48 cfv256 hb272 exf256 big2880 tn1280 nn256 gq384 "
+          "de48 cc512 tg544 pt512 ta512 fof256 yo256 mb_136 sa_32"),
+    (Q8, "wq512 uq128 ur128 vq128 eq512 qx256 qz_128 pqa_160 pqb_160 pqc_160"),
+    (U8, "wp512 us128 uu128 vp128 ep512 sx256 sz_128 ppa_160 ppb_160 ppc_160"),
+]:
+    for _e in _l.split():
+        _k = len(_e.rstrip("0123456789"))
+        for _s in (["0", "1"] if _e[_k - 1] == "_" else [""]):
+            SCRATCH[_e[:_k] + _s] = ("sbuf", [128, int(_e[_k:])], _t)
+SCRATCH["ps"] = ("psum", [128, 4096], F32)
+
+DMAS = ["fn", "x0", "x1", "u", "v", "wc", "ws", "fo", "y0", "y1", "oc0", "oc1", "os0", "os1", "os2", "os3"]
+SEMAPHORES = ["cv", "ca", "cp", "ct", "sent"] + ["d_" + _n for _n in DMAS] + ["arr%d_%d" % (_r, _h) for _r in range(3) for _h in range(2)]
+
+CYC, WAKE, DMA_T, REMOTE_T, ISSUE_T = 0.00104, 0.10, 2.0, 2.5, 0.3
+LEAD0, LEADS, LOOK = 1.0, [-2.0, -2.0, -2.0, -2.0], 0.3
+ENG = ["vvvvvvaaaa", "aaaaaaaaaa"]
+JIT = [0.4 * int(_c) for _c in (
+    "1663842222557777888922481118888027022666619909133336866612333333333222222222251007374444444437333000000009969322333399999999999499999999999990012222798888588840677847443387221111014749822365225002577777777703333233333338888838833336338939018338827477335333341566631143411379988990888199788888888474932444488776222203355556622222444470200500000020000066028112955299222225532307716099995554750095533838405344777770554888774413363430333225993333667800000000812422111177784400577777777399577733330666666660623399713333330330030004333327455666699999999000038469")]
+
+
+def V(name, a, b, s=1):
+    return (name, a, b, s)
+
+
+def cnt(v):
+    return len(range(v[1], v[2], v[3]))
+
+
+def dty(v):
+    return SCRATCH[v[0]][2]
+
+
+def ap(T, v):
+    return T[v[0]][:, v[1]:v[2]] if v[3] == 1 else T[v[0]][:, v[1]:v[2]:v[3]]
+
+
+def build():
+    ops, lead = [], [0.0]
+
+    def add(eng, cost, reads, writes, fn, lat=0.0, sem=None, extra=None, after=(), g=False):
+        ops.append({"eng": eng, "cost": cost, "r": [x for x in reads if isinstance(x, tuple)], "w": writes, "fn": fn,
+                    "lat": lat, "sem": sem, "extra": extra, "after": list(after), "g": bool(g), "lead": lead[0]})
+        return len(ops) - 1
+
+    def sc(T, s):
+        return ap(T, s) if isinstance(s, tuple) else s
+
+    def src(T, v, ind):
+        return ap(T, v).indirect(ap(T, ind)) if ind else ap(T, v)
+
+    def vec(out, ins, more, ind, fn, two=False):
+        n = cnt(out)
+        half = all(SIZE[dty(x)] == 2 for x in [out] + ins)
+        cost = 0.05 + n * 0.0013 if ind else max(64, n * (2 if two else 0.5 if half else 1)) * CYC
+        return add("v", cost, ins + more + [ind], [out], fn, g=ind)
+
+    def cp(out, in_, ind=None):
+        return vec(out, [in_], [], ind, lambda g, T, c: g.vector.tensor_copy(ap(T, out), src(T, in_, ind)))
+
+    def scat(win, ind, in_):
+        return add("v", 0.05 + cnt(in_) * 0.0032, [in_, ind], [win],
+                   lambda g, T, c: g.vector.tensor_copy(ap(T, win).indirect(ap(T, ind)), ap(T, in_)), g=True)
+
+    def tt(out, a, b, op, ind=None):
+        return vec(out, [a, b], [], ind, lambda g, T, c: g.vector.tensor_tensor(ap(T, out), src(T, a, ind), ap(T, b), op), a[0] != "ps")
+
+    def ts(out, a, s1, op0, s2=None, op1=None, ind=None):
+        def fn(g, T, c):
+            if op1 is None:
+                return g.vector.tensor_scalar(ap(T, out), src(T, a, ind), sc(T, s1), None, op0)
+            return g.vector.tensor_scalar(ap(T, out), src(T, a, ind), sc(T, s1), sc(T, s2), op0, op1)
+        return vec(out, [a], [s1, s2], ind, fn)
+
+    def scan(out, d0, d1, op0, op1):
+        return vec(out, [d0, d1], [], None, lambda g, T, c: g.vector.tensor_tensor_scan(ap(T, out), ap(T, d0), ap(T, d1), 0.0, op0, op1))
+
+    def act(out, in_, scale=1.0, bias=None, ind=None, func=None):
+        def fn(g, T, c):
+            if bias is None:
+                return g.scalar.activation(ap(T, out), src(T, in_, ind), func or AF.Copy, scale=sc(T, scale))
+            return g.scalar.activation(ap(T, out), src(T, in_, ind), AF.Identity, bias=sc(T, bias), scale=sc(T, scale))
+        n = cnt(out)
+        return add("a", 0.065 + n * 0.0013 if ind else max(64, n) * CYC, [in_, scale, bias, ind], [out], fn, g=ind)
+
+    def fill(out, val):
+        return act(out, V("ub", 0, cnt(out)), scale=0.0, bias=val)
+
+    def iota(out, pat, base, cm=0):
+        def fn(g, T, c):
+            if dty(out) == I32:
+                return g.iota(ap(T, out), pat, base, cm)
+            return g.iota(ap(T, out), pat, base, cm, allow_small_or_imprecise_dtypes=True)
+        return add("p", 0.16 + 2 * cnt(out) * CYC, [], [out], fn)
+
+    def quant(q, s, in_):
+        return add("v", 0.012 + 0.00022 * cnt(in_), [in_], [q, s], lambda g, T, c: g.vector.quantize_mx(ap(T, q), ap(T, s), ap(T, in_)))
+
+    def mm(bank, lq, lsc, rq, rs, extra=None, after=()):
+        out = V("ps", 512 * bank, 512 * bank + cnt(rq))
+        return add("t", (cnt(rq) + 16) * 0.00125, [lq, lsc, rq, rs], [out],
+                   lambda g, T, c: g.tensor.matmul_mx(ap(T, out), ap(T, lq), ap(T, lsc), ap(T, rq), ap(T, rs), True, True),
+                   extra=extra, after=after)
+
+    def dma(eng, name, reads, writes, fo, fi):
+        return add(eng, 0.06, reads, writes, lambda g, T, c: (g.sync if eng == "s" else g.scalar).dma_start(fo(T), fi(T)),
+                   lat=DMA_T, sem="d_" + name)
+
+    def C(k):
+        return V("bt", 32 * k, 32 * k + 1) if k < 7 else V("col", k, k + 1)
+
+    def W(name, k=0, n=256, stride=256):
+        return V(name, stride * k, stride * k + n)
+
+    dma("s", "fn", [], [W("fni", 0, 16)], lambda T: T.fni[:], lambda T: T.fn[:])
+    dma("s", "u", [], [W("ut", 0, 512)], lambda T: T.ut[:], lambda T: T.u[:])
+    for h in range(2):
+        dma("s", "x%d" % h, [], [V("x_%d" % h, 128, 640)], lambda T, h=h: T["x_%d" % h][:, 128:640], lambda T, h=h: T.x[:, 512 * h:512 * h + 512])
+    dma("s", "wc", [], [W("wq", 0, 512)], lambda T: T.wq[:].bitcast(dt.uint8), lambda T: T.wc[:])
+    dma("s", "ws", [], [W("wp", 0, 512)], lambda T: T.wp[:], lambda T: T.ws[:])
+    dma("s", "v", [], [W("vt", 0, 512)], lambda T: T.vt[:], lambda T: T.v[:])
+
+    B0, B1, B2, B3, R3, R4, BLK, R = range(8)
+    NB0, NB1, NB2, NB3, S16, IS16, IT, S4, T0, ST2, RP16, PB, PBM, PBN, H0, GM, GN = range(8, 25)
+    iota(W("pI", 0, 16), [[0, 16]], 0, 1)
+    iota(W("jj", 0, 33), [[1, 33]], -1)
+    iota(W("ub", 0, RW), [[1, RW]], 1)
+    act(W("ub", 6, RW, RW), W("ub", 0, RW))
+    iota(W("kx", 0, 16), [[16, 16]], 0)
+    ts(W("rI", 0, 16), W("pI", 0, 16), 15, A.bitwise_and)
+    cp(W("cl", 0, 16), W("rI", 0, 16))
+    cp(C(R), W("rI", 0, 1))
+    for k, pat in enumerate([[[0, 16], [1, 2]], [[0, 8], [1, 2], [0, 2]], [[0, 4], [1, 2], [0, 4]], [[0, 2], [1, 2], [0, 8]],
+                             [[0, 8], [1, 4]], [[0, 2], [1, 4], [0, 4]], [[0, 4], [1, 4], [0, 2]]]):
+        iota(W("bi", k, 32, 32), pat, 0)
+    vec(W("bt", 0, 224), [W("bi", 0, 224)], [], None, lambda g, T, c: g.vector.transpose(T.bt[:], T.bi[:]))
+    act(V("col", 8, 12), V("bt", 0, 128, 32), scale=-1.0, bias=1.0)
+    ts(C(S16), C(R), 15.0, A.is_equal, 2.0 ** -10, A.max)
+    ts(V("sm", 0, 16), V("jj", 1, 17), C(R), A.not_equal)
+    ts(V("sm", 16, 32), V("jj", 0, 16), C(R), A.is_equal, 1024.0, A.mult)
+    tt(V("smb", 0, 16), V("sm", 0, 16), V("sm", 16, 32), A.max)
+    act(W("cs", 0, 128), V("smb", 0, 16), ind=V("cl", 0, 8))
+    act(V("smb", 32, 48), V("sm", 0, 16), bias=-1.0)
+    act(V("smb", 48, 64), V("sm", 0, 16), scale=-1.0, bias=1.0)
+    iota(V("dd", 32, 48), [[0, 8], [16, 2]], 0)
+    ts(V("cl", 16, 32), V("dd", 32, 48), C(R), A.add)
+    act(W("tw", 0, 128), V("smb", 32, 64), ind=V("cl", 16, 24))
+    fill(W("seg", 0, 128), 1.0)
+    fill(V("seg", 0, 128, 32), 0.0)
+    iota(V("tab", 0, 4), [[-1, 4]], 1)
+    iota(V("tab", 8, 12, 2), [[1280, 2]], -1024)
+    iota(V("tab", 9, 12, 2), [[0, 2]], 0)
+    iota(V("tab", 16, 20), [[0, 2], [130, 2]], 0)
+    act(C(ST2), V("smb", 48, 49), scale=2.0)
+    act(C(IS16), V("sm", 15, 16), scale=1023.0, bias=1.0)
+    fill(V("kk", 0, 24), 0.0)
+    act(V("kk", 8, 16), V("kx", 0, 8), bias=C(R))
+    act(C(IT), C(R), bias=385.0)
+    ts(W("kd", 0, 8), W("kx", 0, 8), C(IT), A.add, C(IS16), A.mult)
+    fill(V("hb", 0, 272, 136), 0.0)
+    for k in (128, 129):
+        iota(V("uo", k, 1024, 512), [[0, 2]], 130)
+        fill(V("big", k, 20 * RW, RW), 0.0)
+        iota(V("tg", k, 544, 272), [[0, 2]], 0)
+    for k in (1, 2, 3, 4, 5, 7, 8, 9, 10, 11):
+        iota(V("ub", RW * k + 128, RW * k + RW), [[0, 16]], 130)
+    act(C(RP16), C(R), bias=16.0)
+    ts(V("sm", 32, 64), V("jj", 1, 33), C(R), A.is_lt)
+    ts(V("sm", 64, 96), V("jj", 1, 33), C(RP16), A.is_lt, 2048.0, A.mult)
+    tt(V("sm", 96, 128), V("sm", 32, 64), V("sm", 64, 96), A.add)
+    act(V("sm", 128, 144), V("smb", 48, 64))
+    act(V("sm", 144, 160), V("smb", 48, 64), scale=2048.0)
+    for b in range(4):
+        act(W("jb", b, 32, 32), V("sm", 128, 160), scale=128.0 + 32.0 * b)
+        tt(W("big", b, 32, 32), W("jb", b, 32, 32), V("sm", 96, 128), A.add)
+    act(W("gq", 2, 128, 128), V("big", 0, 128))
+    iota(W("nn", 0, 128), [[1, 128]], 0)
+    act(C(PB), C(B3), scale=float(RW))
+    act(C(PBM), C(PB), scale=C(B0))
+    act(C(PBN), C(PB), scale=C(NB0))
+    act(W("big", 5, 128, RW), W("nn", 0, 128), scale=C(B0), bias=C(PBM))
+    act(W("tn", 0, 128), W("nn", 0, 128), scale=C(NB0), bias=C(PBN))
+    iota(W("nn", 1, 128, 128), [[4, 128]], 128)
+    act(C(GM), C(R3), scale=C(B2))
+    act(C(GN), C(R3), scale=C(NB2))
+    act(W("big", 8, 128, RW), W("nn", 1, 128, 128), scale=C(B2), bias=C(GM))
+    act(W("tn", 3, 128, 128), W("nn", 1, 128, 128), scale=C(NB2), bias=C(GN))
+    ts(V("dd", 0, 4), V("jj", 1, 5), C(R4), A.not_equal)
+    ts(V("dd", 4, 8), V("jj", 0, 4), C(R4), A.is_equal, 1024.0, A.mult)
+    tt(V("smb", 64, 68), V("dd", 0, 4), V("dd", 4, 8), A.max)
+    cp(V("cl", 40, 48), V("bt", 32 * R3, 32 * R3 + 8))
+    act(W("cq", 0, 128), V("smb", 64, 68), ind=V("cl", 40, 48))
+    act(C(S4), V("dd", 3, 4), scale=2.0 ** -8 - 4.0, bias=4.0)
+    act(C(T0), C(R3), bias=-4.0)
+    iota(W("cm", 0, 128), [[1, 4], [0, 32]], 0)
+    ts(W("ci", 0, 128), W("cm", 0, 128), C(BLK), A.is_equal)
+    iota(W("cm", 0, 128), [[0, 128]], 0)
+    act(V("cm", 0, 128, 32), V("ci", 0, 128, 32), scale=-BIGC)
+    act(V("cm", 31, 128, 32), V("ci", 0, 128, 32), scale=BIGC)
+    act(C(H0), C(BLK), scale=32.0, bias=32.0)
+    act(V("hc", 2, 4), V("bt", 0, 2), scale=128.0, bias=C(H0))
+    act(V("hc", 0, 2), V("bt", 0, 2), scale=float(RW), bias=C(H0))
+    for h in range(2):
+        iota(V("mb_%d" % h, 0, 1), [[0, 1]], 0)
+        iota(V("y_%d" % h, 0, 128), [[0, 128]], 0)
+        iota(V("p_%d" % h, 128, 512), [[0, 384]], 0)
+    iota(W("et", 0, 516), [[0, 516]], 0)
+    add("p", 0.2 + 2 * 516 * CYC, [W("et", 0, 516)], [W("et", 0, 516)],
+        lambda g, T, c: g.affine_select(T.et[:], T.et[:], [[1, 516]], A.not_equal, 0.5, -3, -4))
+    for b in range(4):
+        quant(W("eq", b, 128, 128), W("ep", b, 128, 128), V("et", 3 - b, 515 - b))
+    quant(W("uq", 0, 128), W("us", 0, 128), W("ut", 0, 512))
+    cp(V("cl", 32, 40), V("kx", 0, 8))
+    add("v", 0.22, [W("uq", 0, 128), V("cl", 32, 40)], [W("ur", 0, 128)],
+        lambda g, T, c: g.vector.tensor_copy(T.ur[:, 0:128].bitcast(dt.uint32), T.uq[:, 0:128].bitcast(dt.uint32).indirect(T.cl[:, 32:40])), g=True)
+    add("a", 0.23, [W("us", 0, 128), V("cl", 32, 40)], [W("uu", 0, 128)],
+        lambda g, T, c: g.scalar.activation(T.uu[:, 0:128], T.us[:, 0:128].indirect(T.cl[:, 32:40]), AF.Copy), g=True)
+    quant(W("vq", 0, 128), W("vp", 0, 128), W("vt", 0, 512))
+
+    for h in range(2):
+        lead[0] = LEAD0 * (1 - h)
+        gat = [act if x == "a" else cp for x in ENG[h]]
+
+        def H(name, k=0, per=1):
+            return W(name, per * h + k, 128, 128)
+
+        def L(name, k=0, per=1):
+            return W(name, per * h + k, 8, 8)
+
+        def UB(k, n=128):
+            return W("ub", 6 * h + k, n, RW)
+
+        def BG(k, n=128):
+            return W("big", k if k in (0, 5, 8) else 10 * h + k, n, RW)
+
+        def TN(k):
+            return W("tn", k if k in (0, 3) else 5 * h + k, 128, 128)
+
+        def extract(lst, row):
+            scan(H("ex"), W("cs", 0, 128), row, A.mult, A.max)
+            ts(lst, V("ex", 128 * h + 15, 128 * h + 128, 16), C(S16), A.mult, -1.0, A.add)
+
+        FL, UL = [L("fl", k, 5) for k in range(5)], [L("ul", k, 5) for k in range(5)]
+        ts(FL[0], L("fni"), -128.0 * h, A.add)
+        r1, ra, rb, ol = H("rf"), H("ra"), H("rb"), L("ol")
+        gat[0](r1, UB(0), ind=FL[0])
+        gat[1](ra, r1, ind=FL[0])
+        extract(FL[1], ra)
+        gat[2](rb, ra, ind=FL[1])
+        extract(FL[2], rb)
+        gat[3](ra, rb, ind=FL[2])
+        extract(FL[3], ra)
+        act(H("tx"), W("tw", 0, 128), ind=FL[3])
+        gat[4](rb, ra, ind=FL[3])
+        extract(FL[4], rb)
+        act(H("ty"), H("tx"), ind=FL[3])
+        gat[5](H("tx"), H("ty"), ind=FL[4])
+        scan(H("smn"), W("seg", 0, 128), H("tx"), A.mult, A.min)
+        scan(H("smx"), W("seg", 0, 128), H("tx"), A.mult, A.max)
+        ts(V("ol", 8 * h, 8 * h + 8, 2), V("smn", 128 * h + 31, 128 * h + 128, 32), -1.0, A.mult, C(ST2), A.add)
+        cp(V("ol", 8 * h + 1, 8 * h + 8, 2), V("smx", 128 * h + 31, 128 * h + 128, 32))
+        uo = W("uo", h, 128, 512)
+        act(H("nc"), V("tab", 0, 4), ind=ol, func=AF.Relu)
+        tt(H("cfv"), V("tab", 8, 12), r1, A.add, ind=ol)
+        tt(uo, V("tab", 16, 20), r1, A.max, ind=ol)
+        ts(L("de", 0, 3), ol, 1.0, A.not_equal)
+        tt(L("de", 1, 3), L("de", 0, 3), W("kd", 0, 8), A.mult)
+        scan(V("hb", 136 * h + 1, 136 * h + 129), H("nc"), H("cfv"), A.mult, A.max)
+        scan(H("exf"), W("cs", 0, 128), W("hb", h, 128, 136), A.mult, A.max)
+        tt(L("de", 2, 3), V("exf", 128 * h + 15, 128 * h + 128, 16), L("de", 1, 3), A.max)
+        ts(L("dl"), L("de", 2, 3), C(S16), A.mult, -1.0, A.add)
+        scat(W("uo", h, 512, 512), L("dl"), r1)
+        extract(UL[0], uo)
+        act(V("fw_%d" % h, 0, 128), uo)
+        rows = [4, 5, 1, 2]
+        for k in range(4):
+            gat[6 + k](UB(rows[k]), UB(rows[k - 1], 130) if k else W("uo", h, 130, 512), ind=UL[k])
+            extract(UL[k + 1], UB(rows[k]))
+        act(UB(3), UB(2, 130), ind=UL[3])
+        for k in range(5):
+            cc = H("cc", k % 2, 2) if k else W("gq", 2, 128, 128)
+            if k:
+                act(cc, BG(k))
+            tt(BG(k + 1) if k < 4 else H("vb"), BG(k, 130), cc, A.add, ind=UL[k])
+        ts(H("tb", 0, 2), H("vb"), 2047, A.bitwise_and)
+        ts(H("tb", 1, 2), H("vb"), 11, A.logical_shift_right)
+        for k in range(3):
+            out = H("pt", k, 2) if k < 2 else H("ta", 0, 2)
+            tt(out, BG(5 + k, 130), TN(k), A.add, ind=UL[k])
+            if k < 2:
+                act(BG(6 + k), out, scale=C(B1 + k))
+                act(TN(k + 1), out, scale=C(NB1 + k))
+        act(H("ta", 1, 2), H("ta", 0, 2), bias=2.0 * RW)
+        tt(H("gq"), BG(8, 130), TN(3), A.add, ind=UL[0])
+        act(BG(9), H("gq"), scale=C(B3))
+        act(TN(4), H("gq"), scale=C(NB3))
+        tt(W("tg", h, 128, 272), BG(9, 130), TN(4), A.add, ind=UL[1])
+        act(V("tg", 272 * h + RW, 272 * h + 272), W("tg", h, 130, 272), ind=UL[2])
+
+    for t in range(4):
+        for h in range(2):
+            def N(s, a, b, st=1):
+                return V("%s_%d" % (s, h), a, b, st)
+
+            def PS(b, n=128):
+                return W("ps", 4 * h + b, n, 512)
+            lead[0] = LEADS[t] * (1 - h)
+            qx, sx = W("qx", h, 128, 128), W("sx", h, 128, 128)
+            quant(qx, sx, N("x", 128, 640))
+            if t == 3:
+                mm(4 * h, W("vq", 0, 128), W("vp", 0, 128), qx, sx)
+                yo = W("yo", h, 128, 128)
+                act(yo, PS(0))
+                dma("a", "y%d" % h, [yo], [], lambda T, h=h: T.y[:, 128 * h:128 * h + 128], lambda T, yo=yo: ap(T, yo))
+                dma("s", "oc%d" % h, [qx], [], lambda T, h=h: T.oc[:, 512 * h:512 * h + 512], lambda T, qx=qx: ap(T, qx).bitcast(dt.uint8))
+                continue
+            for q in (0, 256):
+                act(N("xh", q, 256 + q), N("x", 128 + q, 384 + q), scale=0.5)
+            for q in (0, 256):
+                act(N("xg", q, 256 + q), N("x", 128 + q, 384 + q), scale=0.5)
+            mm(4 * h, W("ur", 0, 128), W("uu", 0, 128), qx, sx)
+            scan(N("mb", 1, 129), W("cm", 0, 128), PS(0), A.add, A.max)
+            tt(N("nf", 0, 128), PS(0), N("mb", 0, 128), A.is_le)
+            scan(N("sh", 0, 128), N("nf", 0, 128), W("ci", 0, 128), A.mult, A.add)
+            ts(N("ho", 0, 4), W("hc", 0, 4), N("sh", 127, 128), A.subtract)
+            cp(N("lp", 0, 16), W("ta", h), ind=N("ho", 2, 3))
+            tt(N("sa", 16, 32), W("tb", h), V("kk", 8, 24), A.max, ind=N("ho", 2, 3))
+            cp(N("ls", 16, 24), N("sa", 16, 24))
+            tt(N("sa", 0, 16), W("tg", h, 272, 272), V("kk", 8, 24), A.max, ind=N("ho", 0, 1))
+            cp(N("ls", 8, 16), N("sa", 0, 8))
+            act(N("fw", 128, 256), W("ub", h, 4 * RW, 6 * RW), ind=N("lp", 0, 8))
+            act(N("fr", 0, 128), N("fw", 0, 256), ind=N("ls", 16, 24))
+            if t == 2:
+                act(W("fof", h, 128, 128), N("fr", 0, 128), bias=128.0 * h - 1.0)
+            scan(N("ez", 0, 128), W("cq", 0, 128), N("fr", 0, 128), A.mult, A.max)
+            ts(N("zl", 0, 32), N("ez", 3, 128, 4), C(S4), A.mult, C(T0), A.add)
+            tt(N("z", 0, 512), N("xh", 0, 512), N("xg", 0, 512), A.add, ind=N("zl", 0, 32))
+            quant(N("qz", 0, 128), N("sz", 0, 128), N("z", 0, 512))
+            act(N("zz", 0, 512), N("z", 0, 512), scale=32.0)
+            for b in range(4):
+                mm(4 * h + b, W("wq", b, 128, 128), W("wp", b, 128, 128), N("qz", 0, 128), N("sz", 0, 128))
+            for b in range(4):
+                tt(N("y", 128 + b, 640, 4), PS(b), N("zz", b, 512, 4), A.add)
+            ts(N("p", 0, 128), N("y", 0, 640), 2.0 ** -5, A.mult, ind=N("ls", 8, 16))
+            pq, pp, arr = "pq%s_%d" % ("abc"[t], h), "pp%s_%d" % ("abc"[t], h), "arr%d_%d" % (t, h)
+            quant(V(pq, 32, 160), V(pp, 32, 160), N("p", 0, 512))
+
+            def send(g, T, c, name, codes, t=t, arr=arr):
+                rid, pid, mask = c[t]
+                o, i = T[name][:, 0:32], T[name][:, 32:64]
+                if codes:
+                    o, i = o.bitcast(dt.uint8), i.bitcast(dt.uint8)
+                g.remote_dma(o, i, T.sem[arr], T.sem.sent, pid, rid, mask)
+            s1 = add("p", ISSUE_T, [V(pq, 32, 64)], [], lambda g, T, c, f=send, n=pq: f(g, T, c, n, True), lat=REMOTE_T, sem="-")
+            s2 = add("p", ISSUE_T, [V(pp, 32, 64)], [], lambda g, T, c, f=send, n=pp: f(g, T, c, n, False), lat=REMOTE_T, sem="-")
+            for q in (0, 256):
+                act(N("x", 128 + q, 384 + q), N("y", 128 + q, 384 + q), scale=2.0 ** -5)
+            act(N("ph", 0, 128), N("p", 0, 128), scale=0.5)
+            for b in range(4):
+                mm(4 * h + b, W("eq", b, 128, 128), W("ep", b, 128, 128), V(pq, 0, 128), V(pp, 0, 128), extra=arr, after=(s1, s2))
+            for b in range(4):
+                tt(N("pn", b, 128, 4), PS(b, 32), N("ph", b, 128, 4), A.add)
+            scat(N("x", 0, 640), N("ls", 8, 16), N("pn", 0, 128))
+    lead[0] = 0.0
+    dma("s", "fo", [W("fof")], [], lambda T: T.fo[:], lambda T: T.fof[0:128:16, :])
+    for k in range(4):
+        dma("sa"[k % 2], "os%d" % k, [W("sx")], [], lambda T, k=k: T.osc[4 * k:4 * k + 4, :], lambda T, k=k: T.sx[32 * k:32 * k + 4, :])
+    return ops
+
+
+def cells(v):
+    return set([v[1] // 512]) if v[0] == "ps" else set(range(v[1], v[2], v[3]))
+
+
+def plan(ops):
+    n = len(ops)
+    hist = {}
+    deps = [set(o["after"]) for o in ops]
+    for i, o in enumerate(ops):
+        acc = [(v, v[0] == "ps") for v in o["r"]] + [(v, True) for v in o["w"]]
+        for v, wr in acc:
+            cs = cells(v)
+            for j, cj, wj in hist.get(v[0], []):
+                if (wr or wj) and not cs.isdisjoint(cj):
+                    deps[i].add(j)
+        for v, wr in acc:
+            hist.setdefault(v[0], []).append((i, cells(v), wr))
+    succ = [[] for _ in ops]
+    for i in range(n):
+        for j in deps[i]:
+            succ[j].append(i)
+    tail = [0.0] * n
+    for i in range(n - 1, -1, -1):
+        tail[i] = ops[i]["cost"] + ops[i]["lat"] + max([WAKE + tail[k] for k in succ[i]] + [0.0])
+    prio = [tail[i] + ops[i]["lead"] + JIT[i % len(JIT)] for i in range(n)]
+    left = [len(d) for d in deps]
+    ready = [i for i in range(n) if left[i] == 0]
+    rt, free = [0.0] * n, {e: 0.0 for e in "vapts"}
+    order, start = [], [0.0] * n
+    while ready:
+        best = None
+        for e in "vapts":
+            cand = [i for i in ready if ops[i]["eng"] == e]
+            if not cand:
+                continue
+            t0 = max(free[e], min(rt[i] for i in cand))
+            i = max([k for k in cand if rt[k] <= t0 + 1e-9], key=lambda k: (prio[k], -k))
+            for k in cand:
+                if t0 < rt[k] < t0 + LOOK * ops[i]["cost"] and prio[k] - prio[i] > ops[k]["cost"]:
+                    i, t0 = k, rt[k]
+            if best is None or t0 < best[0]:
+                best = (t0, i)
+        t0, i = best
+        ready.remove(i)
+        start[i] = t0
+        free[ops[i]["eng"]] = t0 + ops[i]["cost"]
+        order.append(i)
+        for k in succ[i]:
+            rt[k] = max(rt[k], t0 + ops[i]["cost"] + ops[i]["lat"] + WAKE)
+            left[k] -= 1
+            if left[k] == 0:
+                ready.append(k)
+    count = {e: 0 for e in "vapt"}
+    mark, clock, known = [None] * n, [None] * n, {e: {} for e in "vapts"}
+    waits = [{} for _ in ops]
+    pos = {i: k for k, i in enumerate(order)}
+    for i in order:
+        o = ops[i]
+        kn = known[o["eng"]]
+        for j in sorted(deps[i], key=lambda k: -pos[k]):
+            if mark[j] and kn.get(mark[j][0], 0) < mark[j][1]:
+                waits[i][mark[j][0]] = mark[j][1]
+                for s2, v2 in clock[j].items():
+                    kn[s2] = max(kn.get(s2, 0), v2)
+        if o["sem"] is None:
+            count[o["eng"]] += 1
+            mark[i] = ("c" + o["eng"], count[o["eng"]])
+        elif o["sem"] != "-":
+            mark[i] = (o["sem"], 16)
+        clock[i] = dict(kn)
+        if mark[i]:
+            clock[i][mark[i][0]] = mark[i][1]
+    return {"order": order, "waits": waits, "mark": mark, "count": count, "start": start, "deps": deps}
+
+
+CACHE = {}
+
+
+def rank_program(g, core, T, topo):
+    rank = T.rank_of(core)
+    if rank is None:
+        return
+    if not CACHE:
+        CACHE["ops"] = build()
+        CACHE["plan"] = plan(CACHE["ops"])
+    ops, pl = CACHE["ops"], CACHE["plan"]
+    far = min(len(topo.engines(core, T.cores[rank ^ s])) for s in STEP)
+    ctx = []
+    for s in STEP:
+        dst = T.cores[rank ^ s]
+        rid, pid, _ = topo.addr(dst)
+        ctx.append((rid, pid, sum(1 << e for e in topo.engines(core, dst)[:far])))
+    queue = {"v": g.vector, "a": g.scalar, "p": g, "t": g.tensor, "s": g.sync}
+    landed = set()
+    for i in pl["order"]:
+        o = ops[i]
+        q = queue[o["eng"]]
+        for s, val in pl["waits"][i].items():
+            q.wait_ge(T.sem[s], val)
+        if o["extra"] and o["extra"] not in landed:
+            landed.add(o["extra"])
+            q.wait_ge(T.sem[o["extra"]], 2 * far)
+        ins = o["fn"](g, T, ctx)
+        if pl["mark"][i]:
+            ins.then_inc(T.sem[pl["mark"][i][0]], 1 if o["sem"] is None else 16)
+    g.wait_ge(T.sem.sent, 12 * far)
+    for e in "vapt":
+        g.sync.wait_ge(T.sem["c" + e], pl["count"][e])
+    for name in DMAS:
+        g.sync.wait_ge(T.sem["d_" + name], 16)

@@ -7,36 +7,49 @@ SIZE = {F32: 4, BF: 2, I32: 4, U16: 2, Q8: 4, U8: 1}
 STEP = [1, 2, 4]
 RW = 144
 BIGC = 1.0e29
+KP, KS = 512.0, 4096.0
 
-SCRATCH = {}
-for _t, _l in [
-    (I32, "fni16 pI16 rI16 vb256 tb512"),
-    (U16, "cl48 fl80 ul80 ol16 dl16 ho_4 ls_32 lp_16 zl_32"),
-    (BF, "ut512 vt512 et516 smb96 cs128 cq128 tw128 tx256 ty256 seg128 ci128 rf256 ra256 rb256 ex256 smx256 smn256 nc256 uo1024 ub1728 "
-         "x_640 xh_512 xg_512 z_512 zz_512 y_640 p_512 ph_128 pn_128 nf_128 sh_128 fw_256 fr_128 ez_128"),
-    (F32, "col32 bi224 bt224 jj40 kx16 sm160 tab24 kd16 kk24 cm128 jb128 hc8 dd48 cfv256 hb272 exf256 big2880 tn1280 nn256 gq384 "
-          "de48 cc512 tg544 pt512 ta512 fof256 yo256 mb_136 sa_32"),
-    (Q8, "wq512 uq128 ur128 vq128 eq512 qx256 qz_128 pqa_160 pqb_160 pqc_160"),
-    (U8, "wp512 us128 uu128 vp128 ep512 sx256 sz_128 ppa_160 ppb_160 ppc_160"),
+SCRATCH, PLACE = {}, {}
+for _t, _pool, _l in [
+    (I32, "", "fni16 pI8 rI16 vb256 tb_272"),
+    (U16, "", "cl24 fl64 ul64 il16 ho_2 lp_16 rk_16 sl_16"),
+    (BF, "", "ut512 vt512 et516 pz640 x_640 xw_1056 xg_512 z_512 zz_512 y_640 ph_128 pn_128 nf_128 sh_128"),
+    (BF, "kb", "eh128 cc144 cn128 ea128 eb128 smb48 cs128 tw128 da128 db128 tn272 tc272 ci128"),
+    (BF, "hb", "rf_128 ra_128 rb_128 rc_128 ex_128 ma_128 mc_128 sn_128 sx_128 hw_272 rs_128 nc_128 cf_128 po_384"),
+    (BF, "ub", "uo_432"),
+    (BF, "zb", "pp144 pr_432 ta_288 tu_144"),
+    (F32, "", "col48 fof256 yo256 mb_136 sa_32 iw_288"),
+    (F32, "kf", "kx16 kk16 sm160 cm128 jb128 wb128 so128 cd_384 sr_128 pf_16"),
+    (F32, "zf", "wa144 sp144 ck_720 sq_144 tg_288"),
+    (Q8, "", "wq512 uq128 ur128 vq128 eq512 qx256 qz_128 pqa_160 pqb_160 pqc_160"),
+    (U8, "", "wp512 us128 uu128 vp128 ep512 ox256 sz_128 ppa_160 ppb_160 ppc_160"),
 ]:
+    _at = 0
     for _e in _l.split():
         _k = len(_e.rstrip("0123456789"))
         for _s in (["0", "1"] if _e[_k - 1] == "_" else [""]):
-            SCRATCH[_e[:_k] + _s] = ("sbuf", [128, int(_e[_k:])], _t)
+            if _pool:
+                PLACE[_e[:_k] + _s] = (_pool, _at)
+                _at += int(_e[_k:])
+            else:
+                SCRATCH[_e[:_k] + _s] = ("sbuf", [128, int(_e[_k:])], _t)
+    if _pool:
+        SCRATCH[_pool] = ("sbuf", [128, _at], _t)
 SCRATCH["ps"] = ("psum", [128, 4096], F32)
 
 DMAS = ["fn", "x0", "x1", "u", "v", "wc", "ws", "fo", "y0", "y1", "oc0", "oc1", "os0", "os1", "os2", "os3"]
 SEMAPHORES = ["cv", "ca", "cp", "ct", "sent"] + ["d_" + _n for _n in DMAS] + ["arr%d_%d" % (_r, _h) for _r in range(3) for _h in range(2)]
 
-CYC, WAKE, DMA_T, REMOTE_T, ISSUE_T = 0.00104, 0.10, 2.0, 2.5, 0.3
-LEAD0, LEADS, LOOK = 1.0, [-2.0, -2.0, -2.0, -2.0], 0.3
-ENG = ["vvvvvvaaaa", "aaaaaaaaaa"]
+CYC, WAKE, DMA_T, REMOTE_T, ISSUE_T, FIRST_T = 0.00104, 0.19, 1.7, 1.15, 0.2, 1.2
+LOAD_T = {"u": 0.9, "x0": 1.8, "x1": 2.7, "wc": 4.3, "ws": 4.9, "v": 5.8}
+OPT = {'lead0': 0, 'leads': [1, 1, 1, 0], 'look': 0.3, 'const': 2, 'pre': 1, 'f': ['vvvv', 'aaaa'], 'm': ['vavaa', 'aaava'], 'u': ['aaa', 'aaa'], 'copy': ['vaaa', 'pppa'], 'prep': ['aaaa', 'aaaa'], 'late': ['aaaa', 'aaav'], 'xg': 'v', 'xp': 'aaaa', 'pg': 'v', 'yo': 'a'}
 JIT = [0.4 * int(_c) for _c in (
-    "1663842222557777888922481118888027022666619909133336866612333333333222222222251007374444444437333000000009969322333399999999999499999999999990012222798888588840677847443387221111014749822365225002577777777703333233333338888838833336338939018338827477335333341566631143411379988990888199788888888474932444488776222203355556622222444470200500000020000066028112955299222225532307716099995554750095533838405344777770554888774413363430333225993333667800000000812422111177784400577777777399577733330666666660623399713333330330030004333327455666699999999000038469")]
+    "66833339982835551333328772008666651111715713059608077033353339190666647300139333333339499774444028888903888899988885555555555555555822255555555955566666666505553333333329526633333433383371774464755851002611711910334000060900000046553333980880033302444411111115882862222222222277772222100110000034001669999999999999999055555555555555517110969666136667777772222499555555553388351112174009333388333334333333422282282229555430311118882888888866777700004444300000000983322222299677777777777777222222222222222266666633362040777757888867784724222622222668166668666666633533333335555551111888")]
 
 
 def V(name, a, b, s=1):
-    return (name, a, b, s)
+    name, at = PLACE.get(name, (name, 0))
+    return (name, at + a, at + b, s)
 
 
 def cnt(v):
@@ -48,15 +61,21 @@ def dty(v):
 
 
 def ap(T, v):
-    return T[v[0]][:, v[1]:v[2]] if v[3] == 1 else T[v[0]][:, v[1]:v[2]:v[3]]
+    if v[3] == 1:
+        return T[v[0]][:, v[1]:v[2]]
+    return T[v[0]][:, v[1]::v[3]] if v[2] < 0 else T[v[0]][:, v[1]:v[2]:v[3]]
+
+
+def rev(v):
+    return (v[0], v[2] - 1, v[1] - 1, -1)
 
 
 def build():
     ops, lead = [], [0.0]
 
-    def add(eng, cost, reads, writes, fn, lat=0.0, sem=None, extra=None, after=(), g=False):
+    def add(eng, cost, reads, writes, fn, lat=0.0, sem=None, extra=None, after=(), g=0):
         ops.append({"eng": eng, "cost": cost, "r": [x for x in reads if isinstance(x, tuple)], "w": writes, "fn": fn,
-                    "lat": lat, "sem": sem, "extra": extra, "after": list(after), "g": bool(g), "lead": lead[0]})
+                    "lat": lat, "sem": sem, "extra": extra, "after": list(after), "g": g, "lead": lead[0]})
         return len(ops) - 1
 
     def sc(T, s):
@@ -69,14 +88,17 @@ def build():
         n = cnt(out)
         half = all(SIZE[dty(x)] == 2 for x in [out] + ins)
         cost = 0.05 + n * 0.0013 if ind else max(64, n * (2 if two else 0.5 if half else 1)) * CYC
-        return add("v", cost, ins + more + [ind], [out], fn, g=ind)
+        return add("v", cost, ins + more + [ind], [out], fn, g=n if ind else 0)
 
     def cp(out, in_, ind=None):
         return vec(out, [in_], [], ind, lambda g, T, c: g.vector.tensor_copy(ap(T, out), src(T, in_, ind)))
 
+    def mset(out, val):
+        return vec(out, [], [], None, lambda g, T, c: g.vector.memset(ap(T, out), val))
+
     def scat(win, ind, in_):
         return add("v", 0.05 + cnt(in_) * 0.0032, [in_, ind], [win],
-                   lambda g, T, c: g.vector.tensor_copy(ap(T, win).indirect(ap(T, ind)), ap(T, in_)), g=True)
+                   lambda g, T, c: g.vector.tensor_copy(ap(T, win).indirect(ap(T, ind)), ap(T, in_)), g=-cnt(in_))
 
     def tt(out, a, b, op, ind=None):
         return vec(out, [a, b], [], ind, lambda g, T, c: g.vector.tensor_tensor(ap(T, out), src(T, a, ind), ap(T, b), op), a[0] != "ps")
@@ -88,19 +110,16 @@ def build():
             return g.vector.tensor_scalar(ap(T, out), src(T, a, ind), sc(T, s1), sc(T, s2), op0, op1)
         return vec(out, [a], [s1, s2], ind, fn)
 
-    def scan(out, d0, d1, op0, op1):
-        return vec(out, [d0, d1], [], None, lambda g, T, c: g.vector.tensor_tensor_scan(ap(T, out), ap(T, d0), ap(T, d1), 0.0, op0, op1))
+    def scan(out, d0, d1, op0, op1, init=0.0):
+        return vec(out, [d0, d1], [], None, lambda g, T, c: g.vector.tensor_tensor_scan(ap(T, out), ap(T, d0), ap(T, d1), init, op0, op1))
 
-    def act(out, in_, scale=1.0, bias=None, ind=None, func=None):
+    def act(out, in_, scale=1.0, bias=None, ind=None):
         def fn(g, T, c):
             if bias is None:
-                return g.scalar.activation(ap(T, out), src(T, in_, ind), func or AF.Copy, scale=sc(T, scale))
+                return g.scalar.activation(ap(T, out), src(T, in_, ind), AF.Copy, scale=sc(T, scale))
             return g.scalar.activation(ap(T, out), src(T, in_, ind), AF.Identity, bias=sc(T, bias), scale=sc(T, scale))
         n = cnt(out)
-        return add("a", 0.065 + n * 0.0013 if ind else max(64, n) * CYC, [in_, scale, bias, ind], [out], fn, g=ind)
-
-    def fill(out, val):
-        return act(out, V("ub", 0, cnt(out)), scale=0.0, bias=val)
+        return add("a", 0.065 + n * 0.0013 if ind else max(64, n) * CYC, [in_, scale, bias, ind], [out], fn, g=n if ind else 0)
 
     def iota(out, pat, base, cm=0):
         def fn(g, T, c):
@@ -109,8 +128,19 @@ def build():
             return g.iota(ap(T, out), pat, base, cm, allow_small_or_imprecise_dtypes=True)
         return add("p", 0.16 + 2 * cnt(out) * CYC, [], [out], fn)
 
+    def select(out, in_, pat, op, fill, base=0, cm=0):
+        return add("p", 0.21 + 2 * cnt(out) * CYC, [in_], [out],
+                   lambda g, T, c: g.affine_select(ap(T, out), ap(T, in_), pat, op, fill, base, cm))
+
+    def move(e, out, in_, scale=None, ind=None):
+        if e == "p":
+            return select(out, in_, [[0, cnt(out)]], A.is_ge, 0.0)
+        if e == "a":
+            return act(out, in_, 1.0 if scale is None else scale, ind=ind)
+        return cp(out, in_, ind) if scale is None else ts(out, in_, scale, A.mult, ind=ind)
+
     def quant(q, s, in_):
-        return add("v", 0.012 + 0.00022 * cnt(in_), [in_], [q, s], lambda g, T, c: g.vector.quantize_mx(ap(T, q), ap(T, s), ap(T, in_)))
+        return add("v", 0.012 + 0.00022 * cnt(in_), [in_], [q, s], lambda g, T, c: g.vector.quantize_mx(ap(T, q), ap(T, s), ap(T, in_)), g=0.5)
 
     def mm(bank, lq, lsc, rq, rs, extra=None, after=()):
         out = V("ps", 512 * bank, 512 * bank + cnt(rq))
@@ -120,12 +150,12 @@ def build():
 
     def dma(eng, name, reads, writes, fo, fi):
         return add(eng, 0.06, reads, writes, lambda g, T, c: (g.sync if eng == "s" else g.scalar).dma_start(fo(T), fi(T)),
-                   lat=DMA_T, sem="d_" + name)
+                   lat=DMA_T + LOAD_T.get(name, 0.0), sem="d_" + name)
 
-    def C(k):
-        return V("bt", 32 * k, 32 * k + 1) if k < 7 else V("col", k, k + 1)
+    def C(k, n=1):
+        return V("col", k, k + n)
 
-    def W(name, k=0, n=256, stride=256):
+    def W(name, k=0, n=128, stride=128):
         return V(name, stride * k, stride * k + n)
 
     dma("s", "fn", [], [W("fni", 0, 16)], lambda T: T.fni[:], lambda T: T.fn[:])
@@ -136,182 +166,153 @@ def build():
     dma("s", "ws", [], [W("wp", 0, 512)], lambda T: T.wp[:], lambda T: T.ws[:])
     dma("s", "v", [], [W("vt", 0, 512)], lambda T: T.vt[:], lambda T: T.v[:])
 
-    B0, B1, B2, B3, R3, R4, BLK, R = range(8)
-    NB0, NB1, NB2, NB3, S16, IS16, IT, S4, T0, ST2, RP16, PB, PBM, PBN, H0, GM, GN = range(8, 25)
-    iota(W("pI", 0, 16), [[0, 16]], 0, 1)
-    iota(W("jj", 0, 33), [[1, 33]], -1)
-    iota(W("ub", 0, RW), [[1, RW]], 1)
-    act(W("ub", 6, RW, RW), W("ub", 0, RW))
+    B0, B1, B2, B3, R3, BLK, R = range(7)
+    K0, F0, G2, H2, Q2 = 8, 12, 16, 18, 20
+    S16, R1, R16, DA, DB, UNP, SCL, UNS, H0, HC, RS, T0, R128 = range(22, 35)
+    lead[0] = OPT["const"]
+    iota(W("pI", 0, 8), [[0, 8]], 0, 1)
+    iota(W("cc", 0, 130), [[1, 130]], 1)
+    iota(W("eh"), [[0, 4], [1, 32]], 0)
     iota(W("kx", 0, 16), [[16, 16]], 0)
-    ts(W("rI", 0, 16), W("pI", 0, 16), 15, A.bitwise_and)
-    cp(W("cl", 0, 16), W("rI", 0, 16))
-    cp(C(R), W("rI", 0, 1))
-    for k, pat in enumerate([[[0, 16], [1, 2]], [[0, 8], [1, 2], [0, 2]], [[0, 4], [1, 2], [0, 4]], [[0, 2], [1, 2], [0, 8]],
-                             [[0, 8], [1, 4]], [[0, 2], [1, 4], [0, 4]], [[0, 4], [1, 4], [0, 2]]]):
-        iota(W("bi", k, 32, 32), pat, 0)
-    vec(W("bt", 0, 224), [W("bi", 0, 224)], [], None, lambda g, T, c: g.vector.transpose(T.bt[:], T.bi[:]))
-    act(V("col", 8, 12), V("bt", 0, 128, 32), scale=-1.0, bias=1.0)
+    ts(V("rI", 8, 16), W("pI", 0, 8), 15, A.bitwise_and)
+    cp(V("cl", 0, 8), V("rI", 8, 16))
+    cp(C(R), V("rI", 8, 9))
+    for k, (s, m) in enumerate([(0, 1), (1, 1), (2, 1), (3, 1), (0, 3), (1, 3)]):
+        ts(V("rI", k, k + 1), V("pI", 0, 1), s, A.logical_shift_right, m, A.bitwise_and)
+    cp(C(B0, 6), V("rI", 0, 6))
     ts(C(S16), C(R), 15.0, A.is_equal, 2.0 ** -10, A.max)
-    ts(V("sm", 0, 16), V("jj", 1, 17), C(R), A.not_equal)
-    ts(V("sm", 16, 32), V("jj", 0, 16), C(R), A.is_equal, 1024.0, A.mult)
-    tt(V("smb", 0, 16), V("sm", 0, 16), V("sm", 16, 32), A.max)
-    act(W("cs", 0, 128), V("smb", 0, 16), ind=V("cl", 0, 8))
-    act(V("smb", 32, 48), V("sm", 0, 16), bias=-1.0)
-    act(V("smb", 48, 64), V("sm", 0, 16), scale=-1.0, bias=1.0)
-    iota(V("dd", 32, 48), [[0, 8], [16, 2]], 0)
-    ts(V("cl", 16, 32), V("dd", 32, 48), C(R), A.add)
-    act(W("tw", 0, 128), V("smb", 32, 64), ind=V("cl", 16, 24))
-    fill(W("seg", 0, 128), 1.0)
-    fill(V("seg", 0, 128, 32), 0.0)
-    iota(V("tab", 0, 4), [[-1, 4]], 1)
-    iota(V("tab", 8, 12, 2), [[1280, 2]], -1024)
-    iota(V("tab", 9, 12, 2), [[0, 2]], 0)
-    iota(V("tab", 16, 20), [[0, 2], [130, 2]], 0)
-    act(C(ST2), V("smb", 48, 49), scale=2.0)
-    act(C(IS16), V("sm", 15, 16), scale=1023.0, bias=1.0)
-    fill(V("kk", 0, 24), 0.0)
-    act(V("kk", 8, 16), V("kx", 0, 8), bias=C(R))
-    act(C(IT), C(R), bias=385.0)
-    ts(W("kd", 0, 8), W("kx", 0, 8), C(IT), A.add, C(IS16), A.mult)
-    fill(V("hb", 0, 272, 136), 0.0)
-    for k in (128, 129):
-        iota(V("uo", k, 1024, 512), [[0, 2]], 130)
-        fill(V("big", k, 20 * RW, RW), 0.0)
-        iota(V("tg", k, 544, 272), [[0, 2]], 0)
-    for k in (1, 2, 3, 4, 5, 7, 8, 9, 10, 11):
-        iota(V("ub", RW * k + 128, RW * k + RW), [[0, 16]], 130)
-    act(C(RP16), C(R), bias=16.0)
-    ts(V("sm", 32, 64), V("jj", 1, 33), C(R), A.is_lt)
-    ts(V("sm", 64, 96), V("jj", 1, 33), C(RP16), A.is_lt, 2048.0, A.mult)
-    tt(V("sm", 96, 128), V("sm", 32, 64), V("sm", 64, 96), A.add)
-    act(V("sm", 128, 144), V("smb", 48, 64))
-    act(V("sm", 144, 160), V("smb", 48, 64), scale=2048.0)
+    act(C(R1), C(R), bias=1.0)
+    act(C(R16), C(R), bias=16.0)
+    act(C(DA), C(R), bias=-129.0)
+    act(C(DB), C(R), scale=-1.0, bias=113.0)
+    ts(V("smb", 16, 32), V("eh", 0, 16), C(R), A.not_equal)
+    ts(V("smb", 32, 48), V("eh", 0, 16), C(R1), A.is_equal, 1024.0, A.mult)
+    tt(V("smb", 0, 16), V("smb", 16, 32), V("smb", 32, 48), A.max)
+    act(W("cs"), V("smb", 0, 16), ind=V("cl", 0, 8))
+    ts(W("ea"), W("eh"), C(R), A.is_equal)
+    ts(W("eb"), W("eh"), C(R16), A.is_equal)
+    tt(W("tw"), W("eb"), W("ea"), A.subtract)
+    act(W("cn"), W("cc"), scale=-1.0, bias=257.0)
+    mset(W("da"), -1024.0)
+    act(V("da", 0, 128, 32), V("cc", 0, 128, 32), bias=C(DA))
+    mset(W("db"), 1024.0)
+    act(V("db", 0, 128, 32), V("cc", 0, 128, 32), scale=-1.0, bias=C(DB))
+    for name, val in (("tn", 1.0), ("tc", -128.0)):
+        mset(V(name, 0, 129), 0.0)
+        mset(V(name, 129, 257), val)
+    act(C(K0, 4), C(B0, 4), scale=KP)
+    act(C(F0, 4), C(B0, 4), scale=1.0 / KP - 1.0, bias=1.0)
+    ts(C(T0), C(F0), C(F0 + 1), A.mult, C(F0 + 2), A.mult)
+    ts(C(UNP), C(T0), C(F0 + 3), A.mult)
+    act(C(G2, 2), C(B2, 2), scale=KS)
+    act(C(H2, 2), C(B2, 2), scale=KS - 1.0, bias=1.0)
+    act(C(Q2, 2), C(B2, 2), scale=1.0 / KS - 1.0, bias=1.0)
+    ts(C(SCL), C(H2), C(H2 + 1), A.mult)
+    ts(C(UNS), C(Q2), C(Q2 + 1), A.mult)
+    act(C(RS), C(R), scale=C(SCL))
+    act(W("kk", 0, 16), W("kx", 0, 16), scale=C(SCL), bias=C(RS))
+    act(W("pp"), W("cc"), scale=C(K0))
+    act(C(R128), C(R3), bias=124.0)
+    act(W("so"), W("cc"), scale=4.0, bias=C(R128))
+    act(W("sp"), W("so"), scale=C(G2))
+    for name, val in (("ub", 130.0), ("zb", 0.0), ("zf", 0.0)):
+        mset(V(name, 129, SCRATCH[name][1][1], RW), val)
+    ts(V("sm", 0, 32), V("eh", 0, 32), C(R), A.is_lt)
+    ts(V("sm", 32, 64), V("eh", 0, 32), C(R16), A.is_lt, 2048.0, A.mult)
+    tt(V("sm", 64, 96), V("sm", 0, 32), V("sm", 32, 64), A.add)
+    act(V("sm", 96, 128), V("eb", 0, 32), scale=2048.0)
+    tt(V("sm", 128, 160), V("sm", 96, 128), V("ea", 0, 32), A.add)
     for b in range(4):
-        act(W("jb", b, 32, 32), V("sm", 128, 160), scale=128.0 + 32.0 * b)
-        tt(W("big", b, 32, 32), W("jb", b, 32, 32), V("sm", 96, 128), A.add)
-    act(W("gq", 2, 128, 128), V("big", 0, 128))
-    iota(W("nn", 0, 128), [[1, 128]], 0)
-    act(C(PB), C(B3), scale=float(RW))
-    act(C(PBM), C(PB), scale=C(B0))
-    act(C(PBN), C(PB), scale=C(NB0))
-    act(W("big", 5, 128, RW), W("nn", 0, 128), scale=C(B0), bias=C(PBM))
-    act(W("tn", 0, 128), W("nn", 0, 128), scale=C(NB0), bias=C(PBN))
-    iota(W("nn", 1, 128, 128), [[4, 128]], 128)
-    act(C(GM), C(R3), scale=C(B2))
-    act(C(GN), C(R3), scale=C(NB2))
-    act(W("big", 8, 128, RW), W("nn", 1, 128, 128), scale=C(B2), bias=C(GM))
-    act(W("tn", 3, 128, 128), W("nn", 1, 128, 128), scale=C(NB2), bias=C(GN))
-    ts(V("dd", 0, 4), V("jj", 1, 5), C(R4), A.not_equal)
-    ts(V("dd", 4, 8), V("jj", 0, 4), C(R4), A.is_equal, 1024.0, A.mult)
-    tt(V("smb", 64, 68), V("dd", 0, 4), V("dd", 4, 8), A.max)
-    cp(V("cl", 40, 48), V("bt", 32 * R3, 32 * R3 + 8))
-    act(W("cq", 0, 128), V("smb", 64, 68), ind=V("cl", 40, 48))
-    act(C(S4), V("dd", 3, 4), scale=2.0 ** -8 - 4.0, bias=4.0)
-    act(C(T0), C(R3), bias=-4.0)
-    iota(W("cm", 0, 128), [[1, 4], [0, 32]], 0)
-    ts(W("ci", 0, 128), W("cm", 0, 128), C(BLK), A.is_equal)
-    iota(W("cm", 0, 128), [[0, 128]], 0)
+        act(W("jb", b, 32, 32), V("sm", 128, 160), scale=160.0 + 32.0 * b)
+        tt(W("wa", b, 32, 32), W("jb", b, 32, 32), V("sm", 64, 96), A.add)
+    move("p", W("wb"), W("wa"))
+    iota(W("nf_0"), [[1, 4], [0, 32]], 0)
+    ts(W("ci"), W("nf_0"), C(BLK), A.is_equal)
+    mset(W("cm"), 0.0)
     act(V("cm", 0, 128, 32), V("ci", 0, 128, 32), scale=-BIGC)
     act(V("cm", 31, 128, 32), V("ci", 0, 128, 32), scale=BIGC)
     act(C(H0), C(BLK), scale=32.0, bias=32.0)
-    act(V("hc", 2, 4), V("bt", 0, 2), scale=128.0, bias=C(H0))
-    act(V("hc", 0, 2), V("bt", 0, 2), scale=float(RW), bias=C(H0))
+    act(C(HC), C(B0), scale=float(RW), bias=C(H0))
     for h in range(2):
         iota(V("mb_%d" % h, 0, 1), [[0, 1]], 0)
         iota(V("y_%d" % h, 0, 128), [[0, 128]], 0)
-        iota(V("p_%d" % h, 128, 512), [[0, 384]], 0)
-    iota(W("et", 0, 516), [[0, 516]], 0)
-    add("p", 0.2 + 2 * 516 * CYC, [W("et", 0, 516)], [W("et", 0, 516)],
-        lambda g, T, c: g.affine_select(T.et[:], T.et[:], [[1, 516]], A.not_equal, 0.5, -3, -4))
+        iota(V("hw_%d" % h, 128, 129), [[0, 1]], 130)
+        iota(V("pf_%d" % h, 8, 16), [[0, 8]], 0)
+        iota(V("iw_%d" % h, 32, 160), [[1, 128]], 128 * h)
+    iota(V("pz", 128, 512), [[0, 384]], 0)
+    mset(W("et", 0, 516), 0.0)
+    select(W("et", 0, 516), W("et", 0, 516), [[1, 516]], A.not_equal, 0.5, -3, -4)
     for b in range(4):
-        quant(W("eq", b, 128, 128), W("ep", b, 128, 128), V("et", 3 - b, 515 - b))
-    quant(W("uq", 0, 128), W("us", 0, 128), W("ut", 0, 512))
-    cp(V("cl", 32, 40), V("kx", 0, 8))
-    add("v", 0.22, [W("uq", 0, 128), V("cl", 32, 40)], [W("ur", 0, 128)],
-        lambda g, T, c: g.vector.tensor_copy(T.ur[:, 0:128].bitcast(dt.uint32), T.uq[:, 0:128].bitcast(dt.uint32).indirect(T.cl[:, 32:40])), g=True)
-    add("a", 0.23, [W("us", 0, 128), V("cl", 32, 40)], [W("uu", 0, 128)],
-        lambda g, T, c: g.scalar.activation(T.uu[:, 0:128], T.us[:, 0:128].indirect(T.cl[:, 32:40]), AF.Copy), g=True)
-    quant(W("vq", 0, 128), W("vp", 0, 128), W("vt", 0, 512))
+        quant(W("eq", b), W("ep", b), V("et", 3 - b, 515 - b))
+    quant(W("uq"), W("us"), W("ut", 0, 512))
+    cp(V("cl", 16, 24), V("kx", 0, 8))
+    add("v", 0.22, [W("uq"), V("cl", 16, 24)], [W("ur")],
+        lambda g, T, c: g.vector.tensor_copy(T.ur[:, 0:128].bitcast(dt.uint32), T.uq[:, 0:128].bitcast(dt.uint32).indirect(T.cl[:, 16:24])), g=128)
+    add("a", 0.23, [W("us"), V("cl", 16, 24)], [W("uu")],
+        lambda g, T, c: g.scalar.activation(T.uu[:, 0:128], T.us[:, 0:128].indirect(T.cl[:, 16:24]), AF.Copy), g=128)
+    quant(W("vq"), W("vp"), W("vt", 0, 512))
 
     for h in range(2):
-        lead[0] = LEAD0 * (1 - h)
-        gat = [act if x == "a" else cp for x in ENG[h]]
+        lead[0] = OPT["lead0"] * (1 - h)
 
-        def H(name, k=0, per=1):
-            return W(name, per * h + k, 128, 128)
+        def H(name, k=0, n=128, stride=RW):
+            return W("%s_%d" % (name, h), k, n, stride)
 
-        def L(name, k=0, per=1):
-            return W(name, per * h + k, 8, 8)
-
-        def UB(k, n=128):
-            return W("ub", 6 * h + k, n, RW)
-
-        def BG(k, n=128):
-            return W("big", k if k in (0, 5, 8) else 10 * h + k, n, RW)
-
-        def TN(k):
-            return W("tn", k if k in (0, 3) else 5 * h + k, 128, 128)
+        def N(s, a, b, st=1):
+            return V("%s_%d" % (s, h), a, b, st)
 
         def extract(lst, row):
-            scan(H("ex"), W("cs", 0, 128), row, A.mult, A.max)
-            ts(lst, V("ex", 128 * h + 15, 128 * h + 128, 16), C(S16), A.mult, -1.0, A.add)
+            scan(H("ex"), W("cs"), row, A.mult, A.max)
+            ts(lst, N("ex", 15, 128, 16), C(S16), A.mult, -1.0, A.add)
 
-        FL, UL = [L("fl", k, 5) for k in range(5)], [L("ul", k, 5) for k in range(5)]
-        ts(FL[0], L("fni"), -128.0 * h, A.add)
-        r1, ra, rb, ol = H("rf"), H("ra"), H("rb"), L("ol")
-        gat[0](r1, UB(0), ind=FL[0])
-        gat[1](ra, r1, ind=FL[0])
-        extract(FL[1], ra)
-        gat[2](rb, ra, ind=FL[1])
-        extract(FL[2], rb)
-        gat[3](ra, rb, ind=FL[2])
-        extract(FL[3], ra)
-        act(H("tx"), W("tw", 0, 128), ind=FL[3])
-        gat[4](rb, ra, ind=FL[3])
-        extract(FL[4], rb)
-        act(H("ty"), H("tx"), ind=FL[3])
-        gat[5](H("tx"), H("ty"), ind=FL[4])
-        scan(H("smn"), W("seg", 0, 128), H("tx"), A.mult, A.min)
-        scan(H("smx"), W("seg", 0, 128), H("tx"), A.mult, A.max)
-        ts(V("ol", 8 * h, 8 * h + 8, 2), V("smn", 128 * h + 31, 128 * h + 128, 32), -1.0, A.mult, C(ST2), A.add)
-        cp(V("ol", 8 * h + 1, 8 * h + 8, 2), V("smx", 128 * h + 31, 128 * h + 128, 32))
-        uo = W("uo", h, 128, 512)
-        act(H("nc"), V("tab", 0, 4), ind=ol, func=AF.Relu)
-        tt(H("cfv"), V("tab", 8, 12), r1, A.add, ind=ol)
-        tt(uo, V("tab", 16, 20), r1, A.max, ind=ol)
-        ts(L("de", 0, 3), ol, 1.0, A.not_equal)
-        tt(L("de", 1, 3), L("de", 0, 3), W("kd", 0, 8), A.mult)
-        scan(V("hb", 136 * h + 1, 136 * h + 129), H("nc"), H("cfv"), A.mult, A.max)
-        scan(H("exf"), W("cs", 0, 128), W("hb", h, 128, 136), A.mult, A.max)
-        tt(L("de", 2, 3), V("exf", 128 * h + 15, 128 * h + 128, 16), L("de", 1, 3), A.max)
-        ts(L("dl"), L("de", 2, 3), C(S16), A.mult, -1.0, A.add)
-        scat(W("uo", h, 512, 512), L("dl"), r1)
-        extract(UL[0], uo)
-        act(V("fw_%d" % h, 0, 128), uo)
-        rows = [4, 5, 1, 2]
+        FL, UL = [W("fl", 4 * h + k, 8, 8) for k in range(4)], [W("ul", 4 * h + k, 8, 8) for k in range(4)]
+        il = W("il", h, 8, 8)
+        ts(FL[0], W("fni", h, 8, 8), -128.0 * h, A.add)
+        rows = [W("cc"), H("rf"), H("ra"), H("rb"), H("rc")]
         for k in range(4):
-            gat[6 + k](UB(rows[k]), UB(rows[k - 1], 130) if k else W("uo", h, 130, 512), ind=UL[k])
-            extract(UL[k + 1], UB(rows[k]))
-        act(UB(3), UB(2, 130), ind=UL[3])
-        for k in range(5):
-            cc = H("cc", k % 2, 2) if k else W("gq", 2, 128, 128)
+            move(OPT["f"][h][k], rows[k + 1], rows[k], ind=FL[max(k - 1, 0)])
             if k:
-                act(cc, BG(k))
-            tt(BG(k + 1) if k < 4 else H("vb"), BG(k, 130), cc, A.add, ind=UL[k])
-        ts(H("tb", 0, 2), H("vb"), 2047, A.bitwise_and)
-        ts(H("tb", 1, 2), H("vb"), 11, A.logical_shift_right)
+                extract(FL[k], rows[k + 1])
+        tt(H("ma"), W("tw"), W("cn"), A.mult, ind=FL[0])
+        m0, m1 = H("ma"), H("mc")
+        for k, lst in enumerate([2, 2, 3, 3, 3] if OPT["pre"] else [3, 3, 3, 3]):
+            move(OPT["m"][h][k], m1, m0, ind=FL[lst])
+            m0, m1 = m1, m0
+        scan(H("sn"), W("da"), m0, A.max, A.min, -1024.0)
+        scan(H("sx"), W("db"), m0, A.min, A.max, 1024.0)
+        ts(V("il", 8 * h, 8 * h + 8, 2), N("sn", 31, 128, 32), 257.0, A.add)
+        ts(V("il", 8 * h + 1, 8 * h + 8, 2), N("sx", 31, 128, 32), -1.0, A.mult, 257.0, A.add)
+        move("p", N("hw", 129, 257), H("rf"))
+        select(H("rs"), H("rf"), [[0, 4], [1, 32]], A.not_equal, 258.0)
+        act(H("nc"), V("tn", 0, 257), ind=il)
+        tt(H("cf"), V("tc", 0, 257), H("rs"), A.add, ind=il)
+        scan(rev(H("hw")), rev(H("nc")), rev(H("cf")), A.mult, A.max, 130.0)
+        ts(H("uo"), N("hw", 0, 257), 130.0, A.min, ind=il)
+        extract(UL[0], H("uo"))
         for k in range(3):
-            out = H("pt", k, 2) if k < 2 else H("ta", 0, 2)
-            tt(out, BG(5 + k, 130), TN(k), A.add, ind=UL[k])
-            if k < 2:
-                act(BG(6 + k), out, scale=C(B1 + k))
-                act(TN(k + 1), out, scale=C(NB1 + k))
-        act(H("ta", 1, 2), H("ta", 0, 2), bias=2.0 * RW)
-        tt(H("gq"), BG(8, 130), TN(3), A.add, ind=UL[0])
-        act(BG(9), H("gq"), scale=C(B3))
-        act(TN(4), H("gq"), scale=C(NB3))
-        tt(W("tg", h, 128, 272), BG(9, 130), TN(4), A.add, ind=UL[1])
-        act(V("tg", 272 * h + RW, 272 * h + 272), W("tg", h, 130, 272), ind=UL[2])
+            out = H("uo", k + 1) if k < 2 else H("rc")
+            move(OPT["u"][h][k], out, H("uo", k, 130), ind=UL[k])
+            extract(UL[k + 1], out)
+        ts(N("pf", 0, 8), UL[0], 127.0, A.min, 32.0, A.add)
+        for k in range(4):
+            if k:
+                move(OPT["copy"][h][k], H("cd", k - 1, 128, 128), H("ck", k - 1))
+            tt(H("ck", k), H("ck", k - 1, 130) if k else W("wa", 0, 130), H("cd", k - 1, 128, 128) if k else W("wb"), A.add, ind=UL[k])
+        move(OPT["late"][h][0], H("ck", 4), H("ck", 3, 130), ind=UL[3])
+        tt(W("vb", h), H("ck", 4, 130), H("ck", 3), A.add, ind=UL[3])
+        ts(H("tb", 0), W("vb", h), 2047, A.bitwise_and)
+        ts(H("tb", 1), W("vb", h), 11, A.logical_shift_right)
+        for k in range(4):
+            if k:
+                move(OPT["prep"][h][k], H("pr", k - 1), H("po", k - 1, 128, 128), scale=C(K0 + k))
+            tt(H("po", k, 128, 128) if k < 3 else H("ta"), H("pr", k - 1, 130) if k else W("pp", 0, 130),
+               H("po", k - 1, 128, 128) if k else W("cc"), A.max, ind=UL[k])
+        move(OPT["late"][h][1], H("tu"), H("ta", 0, 130), ind=UL[3])
+        move(OPT["late"][h][2], H("ta", 1), H("tu", 0, 130), ind=UL[3])
+        tt(H("sr"), W("sp", 0, 130), W("so"), A.max, ind=UL[0])
+        move(OPT["prep"][h][0], H("sq"), H("sr"), scale=C(G2 + 1))
+        tt(H("tg"), H("sq", 0, 130), H("sr"), A.max, ind=UL[1])
+        move(OPT["late"][h][3], H("tg", 1), H("tg", 0, 130), ind=UL[2])
 
     for t in range(4):
         for h in range(2):
@@ -320,67 +321,71 @@ def build():
 
             def PS(b, n=128):
                 return W("ps", 4 * h + b, n, 512)
-            lead[0] = LEADS[t] * (1 - h)
-            qx, sx = W("qx", h, 128, 128), W("sx", h, 128, 128)
+            lead[0] = OPT["leads"][t] * (1 - h)
+            qx, sx = W("qx", h), W("ox", h)
             quant(qx, sx, N("x", 128, 640))
             if t == 3:
-                mm(4 * h, W("vq", 0, 128), W("vp", 0, 128), qx, sx)
-                yo = W("yo", h, 128, 128)
-                act(yo, PS(0))
+                mm(4 * h, W("vq"), W("vp"), qx, sx)
+                yo = W("yo", h)
+                move(OPT["yo"], yo, PS(0))
                 dma("a", "y%d" % h, [yo], [], lambda T, h=h: T.y[:, 128 * h:128 * h + 128], lambda T, yo=yo: ap(T, yo))
                 dma("s", "oc%d" % h, [qx], [], lambda T, h=h: T.oc[:, 512 * h:512 * h + 512], lambda T, qx=qx: ap(T, qx).bitcast(dt.uint8))
                 continue
-            for q in (0, 256):
-                act(N("xh", q, 256 + q), N("x", 128 + q, 384 + q), scale=0.5)
-            for q in (0, 256):
-                act(N("xg", q, 256 + q), N("x", 128 + q, 384 + q), scale=0.5)
-            mm(4 * h, W("ur", 0, 128), W("uu", 0, 128), qx, sx)
-            scan(N("mb", 1, 129), W("cm", 0, 128), PS(0), A.add, A.max)
+            for b in range(4):
+                act(N("xw", 32 + 256 * b, 160 + 256 * b), N("x", 128 + b, 640, 4), scale=0.5)
+                if OPT["xg"] == "p":
+                    move("p", N("xg", 128 * b, 128 * b + 128), N("xw", 32 + 256 * b, 160 + 256 * b))
+                else:
+                    move(OPT["xg"], N("xg", 128 * b, 128 * b + 128), N("x", 128 + b, 640, 4), scale=0.5)
+            mm(4 * h, W("ur"), W("uu"), qx, sx)
+            scan(N("mb", 1, 129), W("cm"), PS(0), A.add, A.max)
             tt(N("nf", 0, 128), PS(0), N("mb", 0, 128), A.is_le)
-            scan(N("sh", 0, 128), N("nf", 0, 128), W("ci", 0, 128), A.mult, A.add)
-            ts(N("ho", 0, 4), W("hc", 0, 4), N("sh", 127, 128), A.subtract)
-            cp(N("lp", 0, 16), W("ta", h), ind=N("ho", 2, 3))
-            tt(N("sa", 16, 32), W("tb", h), V("kk", 8, 24), A.max, ind=N("ho", 2, 3))
-            cp(N("ls", 16, 24), N("sa", 16, 24))
-            tt(N("sa", 0, 16), W("tg", h, 272, 272), V("kk", 8, 24), A.max, ind=N("ho", 0, 1))
-            cp(N("ls", 8, 16), N("sa", 0, 8))
-            act(N("fw", 128, 256), W("ub", h, 4 * RW, 6 * RW), ind=N("lp", 0, 8))
-            act(N("fr", 0, 128), N("fw", 0, 256), ind=N("ls", 16, 24))
+            scan(N("sh", 0, 128), N("nf", 0, 128), W("ci"), A.mult, A.add)
+            ho = N("ho", 0, 1)
+            ts(ho, N("sh", 127, 128), -1.0, A.mult, C(HC), A.add)
+            ts(N("lp", 0, 16), N("ta", 0, 272), C(UNP), A.mult, -1.0, A.add, ind=ho)
+            tt(N("sa", 0, 16), N("tb", 0, 272), N("pf", 0, 16), A.max, ind=ho)
+            cp(N("rk", 0, 8), N("sa", 0, 8))
+            tt(N("sa", 16, 32), N("tg", 0, 272), W("kk", 0, 16), A.max, ind=ho)
+            ts(N("sl", 0, 8), N("sa", 16, 24), C(UNS), A.mult)
             if t == 2:
-                act(W("fof", h, 128, 128), N("fr", 0, 128), bias=128.0 * h - 1.0)
-            scan(N("ez", 0, 128), W("cq", 0, 128), N("fr", 0, 128), A.mult, A.max)
-            ts(N("zl", 0, 32), N("ez", 3, 128, 4), C(S4), A.mult, C(T0), A.add)
-            tt(N("z", 0, 512), N("xh", 0, 512), N("xg", 0, 512), A.add, ind=N("zl", 0, 32))
+                act(N("iw", 160, 288), N("iw", 32, 160), ind=N("lp", 0, 8))
+                act(W("fof", h), N("iw", 0, 288), ind=N("rk", 0, 8))
+            for b in range(4):
+                move(OPT["xp"][b], N("xw", 160 + 256 * b, 288 + 256 * b), N("xw", 32 + 256 * b, 160 + 256 * b), ind=N("lp", 0, 8))
+                tt(N("z", b, 512, 4), N("xw", 256 * b, 256 * b + 288), N("xg", 128 * b, 128 * b + 128), A.add, ind=N("rk", 0, 8))
+                act(N("zz", 128 * b, 128 * b + 128), N("z", b, 512, 4), scale=32.0)
             quant(N("qz", 0, 128), N("sz", 0, 128), N("z", 0, 512))
-            act(N("zz", 0, 512), N("z", 0, 512), scale=32.0)
             for b in range(4):
-                mm(4 * h + b, W("wq", b, 128, 128), W("wp", b, 128, 128), N("qz", 0, 128), N("sz", 0, 128))
+                mm(4 * h + b, W("wq", b), W("wp", b), N("qz", 0, 128), N("sz", 0, 128))
             for b in range(4):
-                tt(N("y", 128 + b, 640, 4), PS(b), N("zz", b, 512, 4), A.add)
-            ts(N("p", 0, 128), N("y", 0, 640), 2.0 ** -5, A.mult, ind=N("ls", 8, 16))
+                tt(N("y", 128 + b, 640, 4), PS(b), N("zz", 128 * b, 128 * b + 128), A.add)
+            pt = V("pz", 512 * h, 512 * h + 128)
+            move(OPT["pg"], pt, N("y", 0, 640), scale=2.0 ** -5, ind=N("sl", 0, 8))
             pq, pp, arr = "pq%s_%d" % ("abc"[t], h), "pp%s_%d" % ("abc"[t], h), "arr%d_%d" % (t, h)
-            quant(V(pq, 32, 160), V(pp, 32, 160), N("p", 0, 512))
+            quant(V(pq, 32, 160), V(pp, 32, 160), V("pz", 128 * h, 128 * h + 512))
+            a = 32 + 96 * h
 
-            def send(g, T, c, name, codes, t=t, arr=arr):
+            def send(g, T, c, name, codes, t=t, arr=arr, a=a):
                 rid, pid, mask = c[t]
-                o, i = T[name][:, 0:32], T[name][:, 32:64]
+                o, i = T[name][:, 0:32], T[name][:, a:a + 32]
                 if codes:
                     o, i = o.bitcast(dt.uint8), i.bitcast(dt.uint8)
                 g.remote_dma(o, i, T.sem[arr], T.sem.sent, pid, rid, mask)
-            s1 = add("p", ISSUE_T, [V(pq, 32, 64)], [], lambda g, T, c, f=send, n=pq: f(g, T, c, n, True), lat=REMOTE_T, sem="-")
-            s2 = add("p", ISSUE_T, [V(pp, 32, 64)], [], lambda g, T, c, f=send, n=pp: f(g, T, c, n, False), lat=REMOTE_T, sem="-")
+            s1 = add("p", ISSUE_T + (FIRST_T if t + h == 0 else 0.0), [V(pq, a, a + 32)], [], lambda g, T, c, f=send, n=pq: f(g, T, c, n, True), lat=REMOTE_T, sem="-")
+            s2 = add("p", ISSUE_T, [V(pp, a, a + 32)], [], lambda g, T, c, f=send, n=pp: f(g, T, c, n, False), lat=REMOTE_T, sem="-")
             for q in (0, 256):
                 act(N("x", 128 + q, 384 + q), N("y", 128 + q, 384 + q), scale=2.0 ** -5)
-            act(N("ph", 0, 128), N("p", 0, 128), scale=0.5)
+            act(N("ph", 0, 128), pt, scale=0.5)
             for b in range(4):
-                mm(4 * h + b, W("eq", b, 128, 128), W("ep", b, 128, 128), V(pq, 0, 128), V(pp, 0, 128), extra=arr, after=(s1, s2))
+                mm(4 * h + b, W("eq", b), W("ep", b), V(pq, 0, 128), V(pp, 0, 128), extra=arr, after=(s1, s2))
             for b in range(4):
                 tt(N("pn", b, 128, 4), PS(b, 32), N("ph", b, 128, 4), A.add)
-            scat(N("x", 0, 640), N("ls", 8, 16), N("pn", 0, 128))
+            scat(N("x", 0, 640), N("sl", 0, 8), N("pn", 0, 128))
     lead[0] = 0.0
-    dma("s", "fo", [W("fof")], [], lambda T: T.fo[:], lambda T: T.fof[0:128:16, :])
+    dma("s", "fo", [W("fof", 0, 256)], [], lambda T: T.fo[:], lambda T: T.fof[0:128:16, :])
     for k in range(4):
-        dma("sa"[k % 2], "os%d" % k, [W("sx")], [], lambda T, k=k: T.osc[4 * k:4 * k + 4, :], lambda T, k=k: T.sx[32 * k:32 * k + 4, :])
+        dma("sa"[k % 2], "os%d" % k, [W("ox", 0, 256)], [], lambda T, k=k: T.osc[4 * k:4 * k + 4, :], lambda T, k=k: T.ox[32 * k:32 * k + 4, :])
     return ops
 
 
@@ -388,8 +393,7 @@ def cells(v):
     return set([v[1] // 512]) if v[0] == "ps" else set(range(v[1], v[2], v[3]))
 
 
-def plan(ops):
-    n = len(ops)
+def hazards(ops):
     hist = {}
     deps = [set(o["after"]) for o in ops]
     for i, o in enumerate(ops):
@@ -401,6 +405,11 @@ def plan(ops):
                     deps[i].add(j)
         for v, wr in acc:
             hist.setdefault(v[0], []).append((i, cells(v), wr))
+    return deps
+
+
+def arrange(ops, deps, jit):
+    n = len(ops)
     succ = [[] for _ in ops]
     for i in range(n):
         for j in deps[i]:
@@ -408,26 +417,26 @@ def plan(ops):
     tail = [0.0] * n
     for i in range(n - 1, -1, -1):
         tail[i] = ops[i]["cost"] + ops[i]["lat"] + max([WAKE + tail[k] for k in succ[i]] + [0.0])
-    prio = [tail[i] + ops[i]["lead"] + JIT[i % len(JIT)] for i in range(n)]
+    prio = [tail[i] + ops[i]["lead"] + jit[i % len(jit)] for i in range(n)]
     left = [len(d) for d in deps]
-    ready = [i for i in range(n) if left[i] == 0]
+    ready = {e: [i for i in range(n) if left[i] == 0 and ops[i]["eng"] == e] for e in "vapts"}
     rt, free = [0.0] * n, {e: 0.0 for e in "vapts"}
     order, start = [], [0.0] * n
-    while ready:
+    while len(order) < n:
         best = None
         for e in "vapts":
-            cand = [i for i in ready if ops[i]["eng"] == e]
+            cand = ready[e]
             if not cand:
                 continue
             t0 = max(free[e], min(rt[i] for i in cand))
             i = max([k for k in cand if rt[k] <= t0 + 1e-9], key=lambda k: (prio[k], -k))
             for k in cand:
-                if t0 < rt[k] < t0 + LOOK * ops[i]["cost"] and prio[k] - prio[i] > ops[k]["cost"]:
+                if t0 < rt[k] < t0 + OPT["look"] * ops[i]["cost"] and prio[k] - prio[i] > ops[k]["cost"]:
                     i, t0 = k, rt[k]
             if best is None or t0 < best[0]:
                 best = (t0, i)
         t0, i = best
-        ready.remove(i)
+        ready[ops[i]["eng"]].remove(i)
         start[i] = t0
         free[ops[i]["eng"]] = t0 + ops[i]["cost"]
         order.append(i)
@@ -435,7 +444,14 @@ def plan(ops):
             rt[k] = max(rt[k], t0 + ops[i]["cost"] + ops[i]["lat"] + WAKE)
             left[k] -= 1
             if left[k] == 0:
-                ready.append(k)
+                ready[ops[k]["eng"]].append(k)
+    return order, start
+
+
+def plan(ops):
+    n = len(ops)
+    deps = hazards(ops)
+    order, start = arrange(ops, deps, JIT)
     count = {e: 0 for e in "vapt"}
     mark, clock, known = [None] * n, [None] * n, {e: {} for e in "vapts"}
     waits = [{} for _ in ops]

@@ -5,46 +5,52 @@ AF = ActivationFunctionType
 F32, BF, I32, U16, Q8, U8 = "float32", "bfloat16", "int32", "uint16", "float8_e4m3fn_x4", "uint8"
 SIZE = {F32: 4, BF: 2, I32: 4, U16: 2, Q8: 4, U8: 1}
 STEP = [1, 2, 4]
-RW = 144
 BIGC = 1.0e29
 KP, KS = 512.0, 4096.0
-
+OPT = {"pieces": 2, "pre": 1, "fm": 2, "l4": 1, "two": 1, "xg": 1}
 SCRATCH, PLACE = {}, {}
-for _t, _pool, _l in [
-    (I32, "", "fni16 pI8 rI16 vb256 tb_272"),
-    (U16, "", "cl24 fl64 ul64 il16 ho_2 lp_16 rk_16 sl_16"),
-    (BF, "", "ut512 vt512 et516 pz640 x_640 xw_1056 xg_512 z_512 zz_512 y_640 ph_128 pn_128 nf_128 sh_128"),
-    (BF, "kb", "eh128 cc144 cn128 ea128 eb128 smb48 cs128 tw128 da128 db128 tn272 tc272 ci128"),
-    (BF, "hb", "rf_128 ra_128 rb_128 rc_128 ex_128 ma_128 mc_128 sn_128 sx_128 hw_272 rs_128 nc_128 cf_128 po_384"),
-    (BF, "ub", "uo_432"),
-    (BF, "zb", "pp144 pr_432 ta_288 tu_144"),
-    (F32, "", "col48 fof256 yo256 mb_136 sa_32 iw_288"),
-    (F32, "kf", "kx16 kk16 sm160 cm128 jb128 wb128 so128 cd_384 sr_128 pf_16"),
-    (F32, "zf", "wa144 sp144 ck_720 sq_144 tg_288"),
-    (Q8, "", "wq512 uq128 ur128 vq128 eq512 qx256 qz_128 pqa_160 pqb_160 pqc_160"),
-    (U8, "", "wp512 us128 uu128 vp128 ep512 ox256 sz_128 ppa_160 ppb_160 ppc_160"),
-]:
-    _at = 0
-    for _e in _l.split():
-        _k = len(_e.rstrip("0123456789"))
-        for _s in (["0", "1"] if _e[_k - 1] == "_" else [""]):
-            if _pool:
-                PLACE[_e[:_k] + _s] = (_pool, _at)
-                _at += int(_e[_k:])
-            else:
-                SCRATCH[_e[:_k] + _s] = ("sbuf", [128, int(_e[_k:])], _t)
-    if _pool:
-        SCRATCH[_pool] = ("sbuf", [128, _at], _t)
-SCRATCH["ps"] = ("psum", [128, 4096], F32)
 
+
+def layout():
+    n = 256 // OPT["pieces"]
+    rw = n + 16 + n * OPT["two"]
+    SCRATCH.clear()
+    PLACE.clear()
+    for ty, pool, names in [
+        (I32, "", "fni16 pI8 rI16 dI80 vb256 tb_%d" % (2 * rw)),
+        (U16, "", "cl8 fl80 ul64 il16 ho_2 lp_16 rk_16 sl_16"),
+        (BF, "", "ut512 vt512 et516 pz640 x_640 xw_1056 xg_512 z_512 zz_512 y_640 ph_128 pn_128 nf_128 sh_128"),
+        (BF, "kb", "eh32 sg32 tw32 cc256 cn256 lc256 smb96 cs256 da128 db128 tn272 tc272 ci128"),
+        (BF, "hb", "rf256 ra256 rb256 rc256 rd256 ex256 ma256 mc256 sn256 sx256 hw_272 rs256 nc256 cf256 po768"),
+        (BF, "ub", "uo_%d" % (3 * rw)),
+        (BF, "zb", "pp%d pr_%d ta_%d tu_%d" % (rw, 3 * rw, 2 * rw, rw)),
+        (F32, "", "col48 fof256 yo256 mb_136 sa_32 iw_288"),
+        (F32, "kf", "kx16 kk16 sm160 cm128 jb128 wb256 so256 cd768 sr256 pf_16"),
+        (F32, "zf", "wa%d sp%d ck_%d sq_%d tg_%d" % (rw, rw, 5 * rw, rw, 2 * rw)),
+        (Q8, "", "wq512 uq128 ur128 vq128 eq512 qx256 qz_128 pqa_160 pqb_160 pqc_160"),
+        (U8, "", "wp512 us128 uu128 vp128 ep512 ox256 sz_128 ppa_160 ppb_160 ppc_160"),
+    ]:
+        at = 0
+        for e in names.split():
+            k = len(e.rstrip("0123456789"))
+            for s in (["0", "1"] if e[k - 1] == "_" else [""]):
+                if pool:
+                    PLACE[e[:k] + s] = (pool, at)
+                    at += int(e[k:])
+                else:
+                    SCRATCH[e[:k] + s] = ("sbuf", [128, int(e[k:])], ty)
+        if pool:
+            SCRATCH[pool] = ("sbuf", [128, at], ty)
+    SCRATCH["ps"] = ("psum", [128, 4096], F32)
+
+
+layout()
 DMAS = ["fn", "x0", "x1", "u", "v", "wc", "ws", "fo", "y0", "y1", "oc0", "oc1", "os0", "os1", "os2", "os3"]
 SEMAPHORES = ["cv", "ca", "cp", "ct", "sent"] + ["d_" + _n for _n in DMAS] + ["arr%d_%d" % (_r, _h) for _r in range(3) for _h in range(2)]
 
-CYC, WAKE, DMA_T, REMOTE_T, ISSUE_T, FIRST_T = 0.00104, 0.19, 1.7, 1.15, 0.2, 1.2
-LOAD_T = {"u": 0.9, "x0": 1.8, "x1": 2.7, "wc": 4.3, "ws": 4.9, "v": 5.8}
-OPT = {'lead0': 0, 'leads': [1, 1, 1, 0], 'look': 0.3, 'const': 2, 'pre': 1, 'f': ['vvvv', 'aaaa'], 'm': ['vavaa', 'aaava'], 'u': ['aaa', 'aaa'], 'copy': ['vaaa', 'pppa'], 'prep': ['aaaa', 'aaaa'], 'late': ['aaaa', 'aaav'], 'xg': 'v', 'xp': 'aaaa', 'pg': 'v', 'yo': 'a'}
-JIT = [0.4 * int(_c) for _c in (
-    "66833339982835551333328772008666651111715713059608077033353339190666647300139333333339499774444028888903888899988885555555555555555822255555555955566666666505553333333329526633333433383371774464755851002611711910334000060900000046553333980880033302444411111115882862222222222277772222100110000034001669999999999999999055555555555555517110969666136667777772222499555555553388351112174009333388333334333333422282282229555430311118882888888866777700004444300000000983322222299677777777777777222222222222222266666633362040777757888867784724222622222668166668666666633533333335555551111888")]
+CYC = 0.00104
+QUEUES = "dd493da0000009c3030900c100000000204009mc000093a39911a3900016100da0900000mc90900da13"
+ORDER = "0001020304050607112e152n0809280l130j0z0g2o0m0o0n160d0i1v0y314s1w0r0p0h322z0q0f144t0e0t0s0b300k332p0x4u2u34531z1j173n354v1c3c0v1d364w266j0w1b6m4x0u372h5e1x2310381i124y0c6k392r0a6n4z3d2q6l2t503a832m1t3e1s3b272v2i5154183i3f862a2w551q59522x1u3g56192l218c243h2d298a6s2f57221n8d1o3j1k3k6t1r1e583l3m2j2s1y3o3p1p1g5b842k205a6o8b3q6q2b5d5c8e3r6u1m5g5f6p3s8f2c6v1a255h2g1l3t2y855i6w4f1h3u446r5j4o884g3v455k8g433w5l5v5w663x5m4p4h1f67893y5n465o3z47684i5x405p48695y5q4j4987416a5r425z4k4a6b5s604l6c4b5t4m616d4c4n6f4q624e6e6x4d63726y758h646z5u7865737b766g4r798s7c8m708i7e778j6h8p7g8n7a7h8v8q7i7d7f747k8r7l717m7j8w7n8t8x6i7o8y7t7p8o8k8u908l91958z92947q9396979c7u7v9d98997s7x9b7z7r7w7y9a9f8180829e9h9g9s9u9j9i9l9t9k9n9m9v9w9xbeb7ba9y9zbcbgbb9o9qa0bh9p9rb8a1bda2a4a6bib9a3a5a9bja7bfacbkaaafblada8bqbmagbtbnabbwaibrbzambuaealahbxajc0akbyaqapbvc1c2anaoc5boc6arbpc9c4bscaavc3asawc8c7auaxatcbccb0cgazcdcfb4ceb1b3ayb5chb2clcib6cuckcjcpcocmcwcncrcqcvd0cxcscyd1czedeeeid2emctd3ekegd4enejd5eodcd6efd8epd7dfeheqdddieresdldgeydjf1etdmf4ezeldof7f2dpewf5drdef8dkdqdhd9dndsdtdafadvf9dufef0dwdxf6fdeufifcevfhf3dbfbdydze0fge1ffexfjg9fnfkfpe5foe7fle2fme4e3e6e9e8ebfteafrecfsfqfwfvfxfufzfyg3g0g1g4g5gagdg8gcgbg2g6g7"
 
 
 def V(name, a, b, s=1):
@@ -71,11 +77,14 @@ def rev(v):
 
 
 def build():
-    ops, lead = [], [0.0]
+    ops, part = [], [(-1, -1)]
+    n = 256 // OPT["pieces"]
+    RW, SENT = n + 16 + n * OPT["two"], n + 4
+    WL = SENT + n * OPT["two"]
 
-    def add(eng, cost, reads, writes, fn, lat=0.0, sem=None, extra=None, after=(), g=0):
-        ops.append({"eng": eng, "cost": cost, "r": [x for x in reads if isinstance(x, tuple)], "w": writes, "fn": fn,
-                    "lat": lat, "sem": sem, "extra": extra, "after": list(after), "g": g, "lead": lead[0]})
+    def add(alts, reads, writes, sem=None, extra=None, after=()):
+        ops.append({"alts": alts, "r": [x for x in reads if isinstance(x, tuple)], "w": writes, "sem": sem, "extra": extra,
+                    "after": list(after), "part": part[0]})
         return len(ops) - 1
 
     def sc(T, s):
@@ -84,284 +93,342 @@ def build():
     def src(T, v, ind):
         return ap(T, v).indirect(ap(T, ind)) if ind else ap(T, v)
 
-    def vec(out, ins, more, ind, fn, two=False):
-        n = cnt(out)
+    def vcost(out, ins, ind, two=False):
         half = all(SIZE[dty(x)] == 2 for x in [out] + ins)
-        cost = 0.05 + n * 0.0013 if ind else max(64, n * (2 if two else 0.5 if half else 1)) * CYC
-        return add("v", cost, ins + more + [ind], [out], fn, g=n if ind else 0)
+        return ("g", 0.05, cnt(out)) if ind else ("c", max(64, cnt(out) * (2 if two else 0.5 if half else 1)) * CYC, 0)
+
+    def vec(out, ins, more, ind, fn, two=False):
+        return add({"v": vcost(out, ins, ind, two) + (fn,)}, ins + more + [ind], [out])
 
     def cp(out, in_, ind=None):
         return vec(out, [in_], [], ind, lambda g, T, c: g.vector.tensor_copy(ap(T, out), src(T, in_, ind)))
 
-    def mset(out, val):
-        return vec(out, [], [], None, lambda g, T, c: g.vector.memset(ap(T, out), val))
-
     def scat(win, ind, in_):
-        return add("v", 0.05 + cnt(in_) * 0.0032, [in_, ind], [win],
-                   lambda g, T, c: g.vector.tensor_copy(ap(T, win).indirect(ap(T, ind)), ap(T, in_)), g=-cnt(in_))
+        return add({"v": ("s", 0.05, cnt(in_), lambda g, T, c: g.vector.tensor_copy(ap(T, win).indirect(ap(T, ind)), ap(T, in_)))},
+                   [in_, ind], [win])
 
     def tt(out, a, b, op, ind=None):
         return vec(out, [a, b], [], ind, lambda g, T, c: g.vector.tensor_tensor(ap(T, out), src(T, a, ind), ap(T, b), op), a[0] != "ps")
 
-    def ts(out, a, s1, op0, s2=None, op1=None, ind=None):
+    def tsfn(out, a, s1, op0, s2, op1, ind):
         def fn(g, T, c):
             if op1 is None:
                 return g.vector.tensor_scalar(ap(T, out), src(T, a, ind), sc(T, s1), None, op0)
             return g.vector.tensor_scalar(ap(T, out), src(T, a, ind), sc(T, s1), sc(T, s2), op0, op1)
-        return vec(out, [a], [s1, s2], ind, fn)
+        return fn
+
+    def ts(out, a, s1, op0, s2=None, op1=None, ind=None):
+        return vec(out, [a], [s1, s2], ind, tsfn(out, a, s1, op0, s2, op1, ind))
 
     def scan(out, d0, d1, op0, op1, init=0.0):
         return vec(out, [d0, d1], [], None, lambda g, T, c: g.vector.tensor_tensor_scan(ap(T, out), ap(T, d0), ap(T, d1), init, op0, op1))
 
-    def act(out, in_, scale=1.0, bias=None, ind=None):
-        def fn(g, T, c):
-            if bias is None:
-                return g.scalar.activation(ap(T, out), src(T, in_, ind), AF.Copy, scale=sc(T, scale))
-            return g.scalar.activation(ap(T, out), src(T, in_, ind), AF.Identity, bias=sc(T, bias), scale=sc(T, scale))
-        n = cnt(out)
-        return add("a", 0.065 + n * 0.0013 if ind else max(64, n) * CYC, [in_, scale, bias, ind], [out], fn, g=n if ind else 0)
-
-    def iota(out, pat, base, cm=0):
+    def iotafn(out, pat, base, cm):
         def fn(g, T, c):
             if dty(out) == I32:
                 return g.iota(ap(T, out), pat, base, cm)
             return g.iota(ap(T, out), pat, base, cm, allow_small_or_imprecise_dtypes=True)
-        return add("p", 0.16 + 2 * cnt(out) * CYC, [], [out], fn)
+        return ("c", 0.16 + 2 * cnt(out) * CYC, 0, fn)
 
-    def select(out, in_, pat, op, fill, base=0, cm=0):
-        return add("p", 0.21 + 2 * cnt(out) * CYC, [in_], [out],
-                   lambda g, T, c: g.affine_select(ap(T, out), ap(T, in_), pat, op, fill, base, cm))
+    def iota(out, pat, base, cm=0):
+        return add({"p": iotafn(out, pat, base, cm)}, [], [out])
 
-    def move(e, out, in_, scale=None, ind=None):
-        if e == "p":
-            return select(out, in_, [[0, cnt(out)]], A.is_ge, 0.0)
-        if e == "a":
-            return act(out, in_, 1.0 if scale is None else scale, ind=ind)
-        return cp(out, in_, ind) if scale is None else ts(out, in_, scale, A.mult, ind=ind)
+    def fill(out, val):
+        return add({"v": vcost(out, [], None) + (lambda g, T, c: g.vector.memset(ap(T, out), float(val)),),
+                    "p": iotafn(out, [[0, cnt(out)]], val, 0)}, [], [out])
+
+    def selfn(out, in_, pat, op, val, base, cm):
+        return ("c", 0.21 + 2 * cnt(out) * CYC, 0, lambda g, T, c: g.affine_select(ap(T, out), ap(T, in_), pat, op, val, base, cm))
+
+    def select(out, in_, pat, op, val, base=0, cm=0):
+        return add({"p": selfn(out, in_, pat, op, val, base, cm)}, [in_], [out])
+
+    def lin(out, in_, scale=None, bias=None, ind=None):
+        def afn(g, T, c):
+            s = 1.0 if scale is None else sc(T, scale)
+            if bias is None:
+                return g.scalar.activation(ap(T, out), src(T, in_, ind), AF.Copy, scale=s)
+            return g.scalar.activation(ap(T, out), src(T, in_, ind), AF.Identity, bias=sc(T, bias), scale=s)
+        alts = {"a": (("g", 0.065, cnt(out)) if ind else ("c", max(64, cnt(out)) * CYC, 0)) + (afn,)}
+        if scale is None and bias is None:
+            vfn = lambda g, T, c: g.vector.tensor_copy(ap(T, out), src(T, in_, ind))
+            if not ind and in_[0] != "ps":
+                alts["p"] = selfn(out, in_, [[0, cnt(out)]], A.is_ge, 0.0, 0, 0)
+        elif bias is None:
+            vfn = tsfn(out, in_, scale, A.mult, None, None, ind)
+        elif scale is None:
+            vfn = tsfn(out, in_, bias, A.add, None, None, ind)
+        else:
+            vfn = tsfn(out, in_, scale, A.mult, bias, A.add, ind)
+        alts["v"] = vcost(out, [in_], ind) + (vfn,)
+        return add(alts, [in_, scale, bias, ind], [out])
 
     def quant(q, s, in_):
-        return add("v", 0.012 + 0.00022 * cnt(in_), [in_], [q, s], lambda g, T, c: g.vector.quantize_mx(ap(T, q), ap(T, s), ap(T, in_)), g=0.5)
+        return add({"v": ("q", 0.012 + 0.00022 * cnt(in_), 0, lambda g, T, c: g.vector.quantize_mx(ap(T, q), ap(T, s), ap(T, in_)))},
+                   [in_], [q, s])
 
     def mm(bank, lq, lsc, rq, rs, extra=None, after=()):
         out = V("ps", 512 * bank, 512 * bank + cnt(rq))
-        return add("t", (cnt(rq) + 16) * 0.00125, [lq, lsc, rq, rs], [out],
-                   lambda g, T, c: g.tensor.matmul_mx(ap(T, out), ap(T, lq), ap(T, lsc), ap(T, rq), ap(T, rs), True, True),
-                   extra=extra, after=after)
+        return add({"t": ("t", (cnt(rq) + 16) * 0.00125, 0,
+                          lambda g, T, c: g.tensor.matmul_mx(ap(T, out), ap(T, lq), ap(T, lsc), ap(T, rq), ap(T, rs), True, True))},
+                   [lq, lsc, rq, rs], [out], extra=extra, after=after)
 
-    def dma(eng, name, reads, writes, fo, fi):
-        return add(eng, 0.06, reads, writes, lambda g, T, c: (g.sync if eng == "s" else g.scalar).dma_start(fo(T), fi(T)),
-                   lat=DMA_T + LOAD_T.get(name, 0.0), sem="d_" + name)
+    def dma(name, reads, writes, fo, fi):
+        return add({"s": ("d", 0.06, name, lambda g, T, c: g.sync.dma_start(fo(T), fi(T))),
+                    "a": ("d", 0.06, name, lambda g, T, c: g.scalar.dma_start(fo(T), fi(T)))}, reads, writes, sem="d_" + name)
 
-    def C(k, n=1):
-        return V("col", k, k + n)
+    def C(k, m=1):
+        return V("col", k, k + m)
 
-    def W(name, k=0, n=128, stride=128):
-        return V(name, stride * k, stride * k + n)
+    def W(name, k=0, m=128, stride=128):
+        return V(name, stride * k, stride * k + m)
 
-    dma("s", "fn", [], [W("fni", 0, 16)], lambda T: T.fni[:], lambda T: T.fn[:])
-    dma("s", "u", [], [W("ut", 0, 512)], lambda T: T.ut[:], lambda T: T.u[:])
+    dma("fn", [], [W("fni", 0, 16)], lambda T: T.fni[:], lambda T: T.fn[:])
+    dma("u", [], [W("ut", 0, 512)], lambda T: T.ut[:], lambda T: T.u[:])
     for h in range(2):
-        dma("s", "x%d" % h, [], [V("x_%d" % h, 128, 640)], lambda T, h=h: T["x_%d" % h][:, 128:640], lambda T, h=h: T.x[:, 512 * h:512 * h + 512])
-    dma("s", "wc", [], [W("wq", 0, 512)], lambda T: T.wq[:].bitcast(dt.uint8), lambda T: T.wc[:])
-    dma("s", "ws", [], [W("wp", 0, 512)], lambda T: T.wp[:], lambda T: T.ws[:])
-    dma("s", "v", [], [W("vt", 0, 512)], lambda T: T.vt[:], lambda T: T.v[:])
+        dma("x%d" % h, [], [V("x_%d" % h, 128, 640)], lambda T, h=h: T["x_%d" % h][:, 128:640], lambda T, h=h: T.x[:, 512 * h:512 * h + 512])
+    dma("wc", [], [W("wq", 0, 512)], lambda T: T.wq[:].bitcast(dt.uint8), lambda T: T.wc[:])
+    dma("ws", [], [W("wp", 0, 512)], lambda T: T.wp[:], lambda T: T.ws[:])
+    dma("v", [], [W("vt", 0, 512)], lambda T: T.vt[:], lambda T: T.v[:])
 
     B0, B1, B2, B3, R3, BLK, R = range(7)
     K0, F0, G2, H2, Q2 = 8, 12, 16, 18, 20
-    S16, R1, R16, DA, DB, UNP, SCL, UNS, H0, HC, RS, T0, R128 = range(22, 35)
-    lead[0] = OPT["const"]
-    iota(W("pI", 0, 8), [[0, 8]], 0, 1)
-    iota(W("cc", 0, 130), [[1, 130]], 1)
-    iota(W("eh"), [[0, 4], [1, 32]], 0)
+    S16, R16, DA, DB, UNP, SCL, UNS, H0, RS, T0, R128, HC = range(22, 34)
+    iota(V("dI", 0, 32), [[1, 32]], 128, -1)
+    iota(V("pI", 0, 1), [[0, 1]], 0, 1)
+    iota(V("cc", 0, n), [[1, n]], 1)
+    iota(V("eh", 0, 32), [[1, 32]], 0)
+    iota(V("sg", 0, 32), [[2, 2], [0, 16]], -1)
     iota(W("kx", 0, 16), [[16, 16]], 0)
-    ts(V("rI", 8, 16), W("pI", 0, 8), 15, A.bitwise_and)
-    cp(V("cl", 0, 8), V("rI", 8, 16))
-    cp(C(R), V("rI", 8, 9))
-    for k, (s, m) in enumerate([(0, 1), (1, 1), (2, 1), (3, 1), (0, 3), (1, 3)]):
+    for k, (s, m) in enumerate([(0, 1), (1, 1), (2, 1), (3, 1), (0, 3), (1, 3), (0, 15)]):
         ts(V("rI", k, k + 1), V("pI", 0, 1), s, A.logical_shift_right, m, A.bitwise_and)
-    cp(C(B0, 6), V("rI", 0, 6))
-    ts(C(S16), C(R), 15.0, A.is_equal, 2.0 ** -10, A.max)
-    act(C(R1), C(R), bias=1.0)
-    act(C(R16), C(R), bias=16.0)
-    act(C(DA), C(R), bias=-129.0)
-    act(C(DB), C(R), scale=-1.0, bias=113.0)
-    ts(V("smb", 16, 32), V("eh", 0, 16), C(R), A.not_equal)
-    ts(V("smb", 32, 48), V("eh", 0, 16), C(R1), A.is_equal, 1024.0, A.mult)
-    tt(V("smb", 0, 16), V("smb", 16, 32), V("smb", 32, 48), A.max)
-    act(W("cs"), V("smb", 0, 16), ind=V("cl", 0, 8))
-    ts(W("ea"), W("eh"), C(R), A.is_equal)
-    ts(W("eb"), W("eh"), C(R16), A.is_equal)
-    tt(W("tw"), W("eb"), W("ea"), A.subtract)
-    act(W("cn"), W("cc"), scale=-1.0, bias=257.0)
-    mset(W("da"), -1024.0)
-    act(V("da", 0, 128, 32), V("cc", 0, 128, 32), bias=C(DA))
-    mset(W("db"), 1024.0)
-    act(V("db", 0, 128, 32), V("cc", 0, 128, 32), scale=-1.0, bias=C(DB))
-    for name, val in (("tn", 1.0), ("tc", -128.0)):
-        mset(V(name, 0, 129), 0.0)
-        mset(V(name, 129, 257), val)
-    act(C(K0, 4), C(B0, 4), scale=KP)
-    act(C(F0, 4), C(B0, 4), scale=1.0 / KP - 1.0, bias=1.0)
+    cp(C(B0, 7), V("rI", 0, 7))
+    ts(V("dI", 32, 64), V("dI", 0, 32), 15, A.bitwise_and)
+    ts(V("smb", 0, 32), V("dI", 32, 64), 0.0, A.not_equal)
+    ts(V("smb", 32, 64), V("dI", 32, 64), 1.0, A.is_equal, 1024.0, A.mult)
+    ts(V("smb", 64, 96), V("dI", 32, 64), 0.0, A.is_equal)
+    ts(C(S16), V("smb", 79, 80), 2.0 ** -10, A.max)
+    for k in range(0, 128, 32):
+        tt(V("cs", k, k + 32), V("smb", 0, 32), V("smb", 32, 64), A.max)
+    if n == 256:
+        lin(V("cs", 128, 256), V("cs", 0, 128))
+    lin(C(R16), C(R), bias=16.0)
+    lin(C(DA), C(R), bias=-129.0)
+    lin(C(DB), C(R), scale=-1.0, bias=113.0)
+    tt(V("tw", 0, 32), V("smb", 64, 96), V("sg", 0, 32), A.mult)
+    for h in range(n // 128):
+        lin(W("cn", h), W("cc"), scale=-1.0, bias=257.0)
+    lc = V("cc", 0, n)
+    if n == 256:
+        lc = V("lc", 0, n)
+        lin(lc, V("cn", 0, n), scale=-1.0, bias=257.0)
+    fill(W("da"), -1024)
+    lin(V("da", 0, 128, 32), V("cc", 0, 128, 32), bias=C(DA))
+    fill(W("db"), 1024)
+    lin(V("db", 0, 128, 32), V("cc", 0, 128, 32), scale=-1.0, bias=C(DB))
+    for name, val in (("tn", 1), ("tc", -n)):
+        fill(V(name, 0, 129), 0)
+        fill(V(name, 129, 257), val)
+    lin(C(K0, 4), C(B0, 4), scale=KP)
+    lin(C(F0, 4), C(B0, 4), scale=1.0 / KP - 1.0, bias=1.0)
     ts(C(T0), C(F0), C(F0 + 1), A.mult, C(F0 + 2), A.mult)
-    ts(C(UNP), C(T0), C(F0 + 3), A.mult)
-    act(C(G2, 2), C(B2, 2), scale=KS)
-    act(C(H2, 2), C(B2, 2), scale=KS - 1.0, bias=1.0)
-    act(C(Q2, 2), C(B2, 2), scale=1.0 / KS - 1.0, bias=1.0)
-    ts(C(SCL), C(H2), C(H2 + 1), A.mult)
-    ts(C(UNS), C(Q2), C(Q2 + 1), A.mult)
-    act(C(RS), C(R), scale=C(SCL))
-    act(W("kk", 0, 16), W("kx", 0, 16), scale=C(SCL), bias=C(RS))
-    act(W("pp"), W("cc"), scale=C(K0))
-    act(C(R128), C(R3), bias=124.0)
-    act(W("so"), W("cc"), scale=4.0, bias=C(R128))
-    act(W("sp"), W("so"), scale=C(G2))
-    for name, val in (("ub", 130.0), ("zb", 0.0), ("zf", 0.0)):
-        mset(V(name, 129, SCRATCH[name][1][1], RW), val)
+    lin(C(UNP), C(T0), scale=C(F0 + 3))
+    lin(C(G2, 2), C(B2, 2), scale=KS)
+    lin(C(H2, 2), C(B2, 2), scale=KS - 1.0, bias=1.0)
+    lin(C(Q2, 2), C(B2, 2), scale=1.0 / KS - 1.0, bias=1.0)
+    lin(C(SCL), C(H2), scale=C(H2 + 1))
+    lin(C(UNS), C(Q2), scale=C(Q2 + 1))
+    lin(C(RS), C(R), scale=C(SCL))
+    lin(W("kk", 0, 16), W("kx", 0, 16), scale=C(SCL), bias=C(RS))
+    lin(V("pp", 0, n), lc, scale=C(K0))
+    lin(C(R128), C(R3), bias=124.0)
+    lin(V("so", 0, n), lc, scale=4.0, bias=C(R128))
+    lin(V("sp", 0, n), V("so", 0, n), scale=C(G2))
+    for name, val in (("ub", SENT), ("zb", 0), ("zf", 0)):
+        for k in sorted({SENT, WL}):
+            fill(V(name, k - 1, SCRATCH[name][1][1], RW), val)
     ts(V("sm", 0, 32), V("eh", 0, 32), C(R), A.is_lt)
     ts(V("sm", 32, 64), V("eh", 0, 32), C(R16), A.is_lt, 2048.0, A.mult)
     tt(V("sm", 64, 96), V("sm", 0, 32), V("sm", 32, 64), A.add)
-    act(V("sm", 96, 128), V("eb", 0, 32), scale=2048.0)
-    tt(V("sm", 128, 160), V("sm", 96, 128), V("ea", 0, 32), A.add)
+    lin(V("sm", 128, 144), V("smb", 64, 80))
+    lin(V("sm", 144, 160), V("smb", 80, 96), scale=2048.0)
     for b in range(4):
-        act(W("jb", b, 32, 32), V("sm", 128, 160), scale=160.0 + 32.0 * b)
+        lin(W("jb", b, 32, 32), V("sm", 128, 160), scale=160.0 + 32.0 * b)
         tt(W("wa", b, 32, 32), W("jb", b, 32, 32), V("sm", 64, 96), A.add)
-    move("p", W("wb"), W("wa"))
+    for out in [W("wb")] + ([W("wa", 1), W("wb", 1)] if n == 256 else []):
+        lin(out, W("wa"))
     iota(W("nf_0"), [[1, 4], [0, 32]], 0)
     ts(W("ci"), W("nf_0"), C(BLK), A.is_equal)
-    mset(W("cm"), 0.0)
-    act(V("cm", 0, 128, 32), V("ci", 0, 128, 32), scale=-BIGC)
-    act(V("cm", 31, 128, 32), V("ci", 0, 128, 32), scale=BIGC)
-    act(C(H0), C(BLK), scale=32.0, bias=32.0)
-    act(C(HC), C(B0), scale=float(RW), bias=C(H0))
+    fill(W("cm"), 0)
+    lin(V("cm", 0, 128, 32), V("ci", 0, 128, 32), scale=-BIGC)
+    lin(V("cm", 31, 128, 32), V("ci", 0, 128, 32), scale=BIGC)
+    lin(C(H0), C(BLK), scale=32.0, bias=32.0)
+    lin(C(HC), C(B0), scale=float(RW), bias=C(H0))
+    if n == 256:
+        lin(C(HC + 1), C(HC), bias=128.0)
     for h in range(2):
-        iota(V("mb_%d" % h, 0, 1), [[0, 1]], 0)
-        iota(V("y_%d" % h, 0, 128), [[0, 128]], 0)
-        iota(V("hw_%d" % h, 128, 129), [[0, 1]], 130)
-        iota(V("pf_%d" % h, 8, 16), [[0, 8]], 0)
+        fill(V("mb_%d" % h, 0, 1), 0)
+        fill(V("y_%d" % h, 0, 128), 0)
+        fill(V("hw_%d" % h, 128, 129), SENT)
+        fill(V("pf_%d" % h, 8, 16), 0)
         iota(V("iw_%d" % h, 32, 160), [[1, 128]], 128 * h)
-    iota(V("pz", 128, 512), [[0, 384]], 0)
-    mset(W("et", 0, 516), 0.0)
+    fill(V("pz", 128, 512), 0)
+    fill(W("et", 0, 516), 0)
     select(W("et", 0, 516), W("et", 0, 516), [[1, 516]], A.not_equal, 0.5, -3, -4)
     for b in range(4):
         quant(W("eq", b), W("ep", b), V("et", 3 - b, 515 - b))
     quant(W("uq"), W("us"), W("ut", 0, 512))
-    cp(V("cl", 16, 24), V("kx", 0, 8))
-    add("v", 0.22, [W("uq"), V("cl", 16, 24)], [W("ur")],
-        lambda g, T, c: g.vector.tensor_copy(T.ur[:, 0:128].bitcast(dt.uint32), T.uq[:, 0:128].bitcast(dt.uint32).indirect(T.cl[:, 16:24])), g=128)
-    add("a", 0.23, [W("us"), V("cl", 16, 24)], [W("uu")],
-        lambda g, T, c: g.scalar.activation(T.uu[:, 0:128], T.us[:, 0:128].indirect(T.cl[:, 16:24]), AF.Copy), g=128)
+    cl = V("cl", 0, 8)
+    cp(cl, V("kx", 0, 8))
+    add({"v": ("g", 0.05, 128, lambda g, T, c: g.vector.tensor_copy(
+        T.ur[:, 0:128].bitcast(dt.uint32), T.uq[:, 0:128].bitcast(dt.uint32).indirect(T.cl[:, 0:8])))}, [W("uq"), cl], [W("ur")])
+    add({"a": ("g", 0.065, 128, lambda g, T, c: g.scalar.activation(T.uu[:, 0:128], T.us[:, 0:128].indirect(T.cl[:, 0:8]), AF.Copy))},
+        [W("us"), cl], [W("uu")])
     quant(W("vq"), W("vp"), W("vt", 0, 512))
 
-    for h in range(2):
-        lead[0] = OPT["lead0"] * (1 - h)
+    ts(V("dI", 64, 80), W("fni", 0, 16), 31, A.bitwise_and)
+    cp(W("fl", 4, 16, 16), V("dI", 64, 80))
+    for pc in range(OPT["pieces"]):
+        halves = [pc] if n == 128 else [0, 1]
+        part[0] = (-1, pc)
 
-        def H(name, k=0, n=128, stride=RW):
-            return W("%s_%d" % (name, h), k, n, stride)
+        def H(name, k=0):
+            return V(name, 256 * k + n * pc, 256 * k + n * pc + n)
 
-        def N(s, a, b, st=1):
-            return V("%s_%d" % (s, h), a, b, st)
+        def G(name, k=0, m=n):
+            return W("%s_%d" % (name, pc), k, m, RW)
+
+        def L(name, k):
+            return V(name, 16 * k + n // 16 * pc, 16 * k + n // 16 * (pc + 1))
 
         def extract(lst, row):
-            scan(H("ex"), W("cs"), row, A.mult, A.max)
-            ts(lst, N("ex", 15, 128, 16), C(S16), A.mult, -1.0, A.add)
+            scan(H("ex"), V("cs", 0, n), row, A.mult, A.max)
+            ts(lst, V("ex", n * pc + 15, n * pc + n, 16), C(S16), A.mult, -1.0, A.add)
 
-        FL, UL = [W("fl", 4 * h + k, 8, 8) for k in range(4)], [W("ul", 4 * h + k, 8, 8) for k in range(4)]
-        il = W("il", h, 8, 8)
-        ts(FL[0], W("fni", h, 8, 8), -128.0 * h, A.add)
-        rows = [W("cc"), H("rf"), H("ra"), H("rb"), H("rc")]
-        for k in range(4):
-            move(OPT["f"][h][k], rows[k + 1], rows[k], ind=FL[max(k - 1, 0)])
-            if k:
-                extract(FL[k], rows[k + 1])
-        tt(H("ma"), W("tw"), W("cn"), A.mult, ind=FL[0])
-        m0, m1 = H("ma"), H("mc")
-        for k, lst in enumerate([2, 2, 3, 3, 3] if OPT["pre"] else [3, 3, 3, 3]):
-            move(OPT["m"][h][k], m1, m0, ind=FL[lst])
+        FL, UL = [L("fl", k) for k in range(5)], [L("ul", k) for k in range(4)]
+        ts(FL[0], L("fni", 0), -1.0 * n * pc, A.add)
+        rows = [V("cc", 0, n), H("rf"), H("ra"), H("rb"), H("rc"), H("ra")]
+        if OPT["fm"] == 2:
+            for k in range(4):
+                lin(rows[k + 1], rows[k], ind=FL[max(k - 1, 0)])
+                if k:
+                    extract(FL[k], rows[k + 1])
+            pulls = [2, 2, 3, 3, 3] if OPT["pre"] else [3, 3, 3, 3]
+        else:
+            for k in range(5):
+                lin(rows[k + 1], rows[k], ind=FL[k // 3])
+                if k in (2, 4):
+                    extract(FL[k // 2], rows[k + 1])
+            pulls = [0, 1, 1, 1, 1, 2, 2]
+        tt(H("ma"), V("tw", 0, 32), V("cn", 0, n), A.mult, ind=FL[4])
+        m0, m1 = "ma", "mc"
+        for lst in pulls:
+            lin(H(m1), H(m0), ind=FL[lst])
             m0, m1 = m1, m0
-        scan(H("sn"), W("da"), m0, A.max, A.min, -1024.0)
-        scan(H("sx"), W("db"), m0, A.min, A.max, 1024.0)
-        ts(V("il", 8 * h, 8 * h + 8, 2), N("sn", 31, 128, 32), 257.0, A.add)
-        ts(V("il", 8 * h + 1, 8 * h + 8, 2), N("sx", 31, 128, 32), -1.0, A.mult, 257.0, A.add)
-        move("p", N("hw", 129, 257), H("rf"))
-        select(H("rs"), H("rf"), [[0, 4], [1, 32]], A.not_equal, 258.0)
-        act(H("nc"), V("tn", 0, 257), ind=il)
-        tt(H("cf"), V("tc", 0, 257), H("rs"), A.add, ind=il)
-        scan(rev(H("hw")), rev(H("nc")), rev(H("cf")), A.mult, A.max, 130.0)
-        ts(H("uo"), N("hw", 0, 257), 130.0, A.min, ind=il)
-        extract(UL[0], H("uo"))
+        select(H("rs"), H("rf"), [[0, n // 32], [1, 32]], A.not_equal, float(SENT + n))
+        for h in halves:
+            il, hw = W("il", h, 8, 8), "hw_%d" % h
+            scan(W("sn", h), W("da"), W(m0, h), A.max, A.min, -1024.0)
+            scan(W("sx", h), W("db"), W(m0, h), A.min, A.max, 1024.0)
+            ts(V("il", 8 * h, 8 * h + 8, 2), V("sn", 128 * h + 31, 128 * h + 128, 32), 257.0, A.add)
+            ts(V("il", 8 * h + 1, 8 * h + 8, 2), V("sx", 128 * h + 31, 128 * h + 128, 32), -1.0, A.mult, 257.0, A.add)
+            lin(V(hw, 129, 257), W("rf", h))
+            lin(W("nc", h), V("tn", 0, 257), ind=il)
+            tt(W("cf", h), V("tc", 0, 257), W("rs", h), A.add, ind=il)
+            scan(rev(W(hw)), rev(W("nc", h)), rev(W("cf", h)), A.mult, A.max, float(SENT))
+            if OPT["two"]:
+                lin(W("uo_%d" % pc, h - halves[0]), V(hw, 0, 257), ind=il)
+            else:
+                ts(W("uo_%d" % pc, h - halves[0]), V(hw, 0, 257), float(SENT), A.min, ind=il)
+        extract(UL[0], G("uo"))
         for k in range(3):
-            out = H("uo", k + 1) if k < 2 else H("rc")
-            move(OPT["u"][h][k], out, H("uo", k, 130), ind=UL[k])
+            out = G("uo", k + 1) if k < 2 else H("rd")
+            lin(out, G("uo", k, WL), ind=UL[k])
             extract(UL[k + 1], out)
-        ts(N("pf", 0, 8), UL[0], 127.0, A.min, 32.0, A.add)
+        for h in halves:
+            ts(V("pf_%d" % h, 0, 8), W("ul", h, 8, 8), 32.0 - 128.0 * (h - halves[0]), A.add, 159.0, A.min)
         for k in range(4):
+            if k == 3 and OPT["l4"]:
+                lin(G("ck", 4), G("ck", 2, WL), ind=UL[2])
+                tt(G("ck", 3), G("ck", 4, WL), G("ck", 2), A.add, ind=UL[2])
+                continue
             if k:
-                move(OPT["copy"][h][k], H("cd", k - 1, 128, 128), H("ck", k - 1))
-            tt(H("ck", k), H("ck", k - 1, 130) if k else W("wa", 0, 130), H("cd", k - 1, 128, 128) if k else W("wb"), A.add, ind=UL[k])
-        move(OPT["late"][h][0], H("ck", 4), H("ck", 3, 130), ind=UL[3])
-        tt(W("vb", h), H("ck", 4, 130), H("ck", 3), A.add, ind=UL[3])
-        ts(H("tb", 0), W("vb", h), 2047, A.bitwise_and)
-        ts(H("tb", 1), W("vb", h), 11, A.logical_shift_right)
+                lin(H("cd", k - 1), G("ck", k - 1))
+            tt(G("ck", k), G("ck", k - 1, WL) if k else V("wa", 0, WL), H("cd", k - 1) if k else V("wb", 0, n), A.add, ind=UL[k])
+        lin(G("ck", 4), G("ck", 3, WL), ind=UL[3])
+        tt(H("vb"), G("ck", 4, WL), G("ck", 3), A.add, ind=UL[3])
+        for h in halves:
+            at = 128 * (h - halves[0])
+            ts(V("tb_%d" % pc, at, at + 128), W("vb", h), 2047, A.bitwise_and)
+            ts(V("tb_%d" % pc, RW + at, RW + at + 128), W("vb", h), 11, A.logical_shift_right)
         for k in range(4):
+            if k == 2 and OPT["l4"]:
+                lin(G("pr", 1), H("po", 1), scale=C(K0 + 2))
+                tt(G("tu"), G("pr", 1, WL), H("po", 1), A.max, ind=UL[2])
+                lin(G("pr", 2), G("tu", 0, WL), scale=C(K0 + 3), ind=UL[2])
+                tt(G("ta"), G("pr", 2, WL), G("tu"), A.max, ind=UL[2])
+                break
             if k:
-                move(OPT["prep"][h][k], H("pr", k - 1), H("po", k - 1, 128, 128), scale=C(K0 + k))
-            tt(H("po", k, 128, 128) if k < 3 else H("ta"), H("pr", k - 1, 130) if k else W("pp", 0, 130),
-               H("po", k - 1, 128, 128) if k else W("cc"), A.max, ind=UL[k])
-        move(OPT["late"][h][1], H("tu"), H("ta", 0, 130), ind=UL[3])
-        move(OPT["late"][h][2], H("ta", 1), H("tu", 0, 130), ind=UL[3])
-        tt(H("sr"), W("sp", 0, 130), W("so"), A.max, ind=UL[0])
-        move(OPT["prep"][h][0], H("sq"), H("sr"), scale=C(G2 + 1))
-        tt(H("tg"), H("sq", 0, 130), H("sr"), A.max, ind=UL[1])
-        move(OPT["late"][h][3], H("tg", 1), H("tg", 0, 130), ind=UL[2])
+                lin(G("pr", k - 1), H("po", k - 1), scale=C(K0 + k))
+            tt(H("po", k) if k < 3 else G("ta"), G("pr", k - 1, WL) if k else V("pp", 0, WL), H("po", k - 1) if k else lc, A.max, ind=UL[k])
+        lin(G("tu"), G("ta", 0, WL), ind=UL[3])
+        lin(G("ta", 1), G("tu", 0, WL), ind=UL[3])
+        tt(H("sr"), V("sp", 0, WL), V("so", 0, n), A.max, ind=UL[0])
+        lin(G("sq"), H("sr"), scale=C(G2 + 1))
+        tt(G("tg"), G("sq", 0, WL), H("sr"), A.max, ind=UL[1])
+        lin(G("tg", 1), G("tg", 0, WL), ind=UL[2])
 
     for t in range(4):
         for h in range(2):
             def N(s, a, b, st=1):
                 return V("%s_%d" % (s, h), a, b, st)
 
-            def PS(b, n=128):
-                return W("ps", 4 * h + b, n, 512)
-            lead[0] = OPT["leads"][t] * (1 - h)
+            def PS(b, m=128):
+                return W("ps", 4 * h + b, m, 512)
+
+            def TB(name):
+                return V("%s_%d" % (name, h if n == 128 else 0), 0, RW + n)
+            part[0] = (t, h)
             qx, sx = W("qx", h), W("ox", h)
             quant(qx, sx, N("x", 128, 640))
             if t == 3:
                 mm(4 * h, W("vq"), W("vp"), qx, sx)
                 yo = W("yo", h)
-                move(OPT["yo"], yo, PS(0))
-                dma("a", "y%d" % h, [yo], [], lambda T, h=h: T.y[:, 128 * h:128 * h + 128], lambda T, yo=yo: ap(T, yo))
-                dma("s", "oc%d" % h, [qx], [], lambda T, h=h: T.oc[:, 512 * h:512 * h + 512], lambda T, qx=qx: ap(T, qx).bitcast(dt.uint8))
+                lin(yo, PS(0))
+                dma("y%d" % h, [yo], [], lambda T, h=h: T.y[:, 128 * h:128 * h + 128], lambda T, yo=yo: ap(T, yo))
+                dma("oc%d" % h, [qx], [], lambda T, h=h: T.oc[:, 512 * h:512 * h + 512], lambda T, qx=qx: ap(T, qx).bitcast(dt.uint8))
                 continue
             for b in range(4):
-                act(N("xw", 32 + 256 * b, 160 + 256 * b), N("x", 128 + b, 640, 4), scale=0.5)
-                if OPT["xg"] == "p":
-                    move("p", N("xg", 128 * b, 128 * b + 128), N("xw", 32 + 256 * b, 160 + 256 * b))
+                lin(N("xw", 32 + 256 * b, 160 + 256 * b), N("x", 128 + b, 640, 4), scale=0.5)
+                if OPT["xg"]:
+                    lin(N("xg", 128 * b, 128 * b + 128), N("xw", 32 + 256 * b, 160 + 256 * b))
                 else:
-                    move(OPT["xg"], N("xg", 128 * b, 128 * b + 128), N("x", 128 + b, 640, 4), scale=0.5)
+                    lin(N("xg", 128 * b, 128 * b + 128), N("x", 128 + b, 640, 4), scale=0.5)
             mm(4 * h, W("ur"), W("uu"), qx, sx)
             scan(N("mb", 1, 129), W("cm"), PS(0), A.add, A.max)
             tt(N("nf", 0, 128), PS(0), N("mb", 0, 128), A.is_le)
             scan(N("sh", 0, 128), N("nf", 0, 128), W("ci"), A.mult, A.add)
             ho = N("ho", 0, 1)
-            ts(ho, N("sh", 127, 128), -1.0, A.mult, C(HC), A.add)
-            ts(N("lp", 0, 16), N("ta", 0, 272), C(UNP), A.mult, -1.0, A.add, ind=ho)
-            tt(N("sa", 0, 16), N("tb", 0, 272), N("pf", 0, 16), A.max, ind=ho)
+            ts(ho, N("sh", 127, 128), -1.0, A.mult, C(HC + (h if n == 256 else 0)), A.add)
+            ts(N("lp", 0, 16), TB("ta"), C(UNP), A.mult, -1.0, A.add, ind=ho)
+            tt(N("sa", 0, 16), TB("tb"), N("pf", 0, 16), A.max, ind=ho)
             cp(N("rk", 0, 8), N("sa", 0, 8))
-            tt(N("sa", 16, 32), N("tg", 0, 272), W("kk", 0, 16), A.max, ind=ho)
+            tt(N("sa", 16, 32), TB("tg"), W("kk", 0, 16), A.max, ind=ho)
             ts(N("sl", 0, 8), N("sa", 16, 24), C(UNS), A.mult)
             if t == 2:
-                act(N("iw", 160, 288), N("iw", 32, 160), ind=N("lp", 0, 8))
-                act(W("fof", h), N("iw", 0, 288), ind=N("rk", 0, 8))
+                lin(N("iw", 160, 288), N("iw", 32, 160), ind=N("lp", 0, 8))
+                lin(W("fof", h), N("iw", 0, 288), ind=N("rk", 0, 8))
             for b in range(4):
-                move(OPT["xp"][b], N("xw", 160 + 256 * b, 288 + 256 * b), N("xw", 32 + 256 * b, 160 + 256 * b), ind=N("lp", 0, 8))
+                lin(N("xw", 160 + 256 * b, 288 + 256 * b), N("xw", 32 + 256 * b, 160 + 256 * b), ind=N("lp", 0, 8))
                 tt(N("z", b, 512, 4), N("xw", 256 * b, 256 * b + 288), N("xg", 128 * b, 128 * b + 128), A.add, ind=N("rk", 0, 8))
-                act(N("zz", 128 * b, 128 * b + 128), N("z", b, 512, 4), scale=32.0)
+                lin(N("zz", 128 * b, 128 * b + 128), N("z", b, 512, 4), scale=32.0)
             quant(N("qz", 0, 128), N("sz", 0, 128), N("z", 0, 512))
             for b in range(4):
                 mm(4 * h + b, W("wq", b), W("wp", b), N("qz", 0, 128), N("sz", 0, 128))
             for b in range(4):
                 tt(N("y", 128 + b, 640, 4), PS(b), N("zz", 128 * b, 128 * b + 128), A.add)
             pt = V("pz", 512 * h, 512 * h + 128)
-            move(OPT["pg"], pt, N("y", 0, 640), scale=2.0 ** -5, ind=N("sl", 0, 8))
+            lin(pt, N("y", 0, 640), scale=2.0 ** -5, ind=N("sl", 0, 8))
             pq, pp, arr = "pq%s_%d" % ("abc"[t], h), "pp%s_%d" % ("abc"[t], h), "arr%d_%d" % (t, h)
             quant(V(pq, 32, 160), V(pp, 32, 160), V("pz", 128 * h, 128 * h + 512))
             a = 32 + 96 * h
@@ -372,20 +439,19 @@ def build():
                 if codes:
                     o, i = o.bitcast(dt.uint8), i.bitcast(dt.uint8)
                 g.remote_dma(o, i, T.sem[arr], T.sem.sent, pid, rid, mask)
-            s1 = add("p", ISSUE_T + (FIRST_T if t + h == 0 else 0.0), [V(pq, a, a + 32)], [], lambda g, T, c, f=send, n=pq: f(g, T, c, n, True), lat=REMOTE_T, sem="-")
-            s2 = add("p", ISSUE_T, [V(pp, a, a + 32)], [], lambda g, T, c, f=send, n=pp: f(g, T, c, n, False), lat=REMOTE_T, sem="-")
+            s1 = add({"p": ("r", 0.2, 0, lambda g, T, c, f=send, m=pq: f(g, T, c, m, True))}, [V(pq, a, a + 32)], [], sem="-")
+            s2 = add({"p": ("r", 0.2, 0, lambda g, T, c, f=send, m=pp: f(g, T, c, m, False))}, [V(pp, a, a + 32)], [], sem="-")
             for q in (0, 256):
-                act(N("x", 128 + q, 384 + q), N("y", 128 + q, 384 + q), scale=2.0 ** -5)
-            act(N("ph", 0, 128), pt, scale=0.5)
+                lin(N("x", 128 + q, 384 + q), N("y", 128 + q, 384 + q), scale=2.0 ** -5)
+            lin(N("ph", 0, 128), pt, scale=0.5)
             for b in range(4):
                 mm(4 * h + b, W("eq", b), W("ep", b), V(pq, 0, 128), V(pp, 0, 128), extra=arr, after=(s1, s2))
             for b in range(4):
                 tt(N("pn", b, 128, 4), PS(b, 32), N("ph", b, 128, 4), A.add)
             scat(N("x", 0, 640), N("sl", 0, 8), N("pn", 0, 128))
-    lead[0] = 0.0
-    dma("s", "fo", [W("fof", 0, 256)], [], lambda T: T.fo[:], lambda T: T.fof[0:128:16, :])
+    dma("fo", [W("fof", 0, 256)], [], lambda T: T.fo[:], lambda T: T.fof[0:128:16, :])
     for k in range(4):
-        dma("sa"[k % 2], "os%d" % k, [W("ox", 0, 256)], [], lambda T, k=k: T.osc[4 * k:4 * k + 4, :], lambda T, k=k: T.ox[32 * k:32 * k + 4, :])
+        dma("os%d" % k, [W("ox", 0, 256)], [], lambda T, k=k: T.osc[4 * k:4 * k + 4, :], lambda T, k=k: T.ox[32 * k:32 * k + 4, :])
     return ops
 
 
@@ -408,71 +474,45 @@ def hazards(ops):
     return deps
 
 
-def arrange(ops, deps, jit):
-    n = len(ops)
-    succ = [[] for _ in ops]
-    for i in range(n):
-        for j in deps[i]:
-            succ[j].append(i)
-    tail = [0.0] * n
-    for i in range(n - 1, -1, -1):
-        tail[i] = ops[i]["cost"] + ops[i]["lat"] + max([WAKE + tail[k] for k in succ[i]] + [0.0])
-    prio = [tail[i] + ops[i]["lead"] + jit[i % len(jit)] for i in range(n)]
-    left = [len(d) for d in deps]
-    ready = {e: [i for i in range(n) if left[i] == 0 and ops[i]["eng"] == e] for e in "vapts"}
-    rt, free = [0.0] * n, {e: 0.0 for e in "vapts"}
-    order, start = [], [0.0] * n
-    while len(order) < n:
-        best = None
-        for e in "vapts":
-            cand = ready[e]
-            if not cand:
-                continue
-            t0 = max(free[e], min(rt[i] for i in cand))
-            i = max([k for k in cand if rt[k] <= t0 + 1e-9], key=lambda k: (prio[k], -k))
-            for k in cand:
-                if t0 < rt[k] < t0 + OPT["look"] * ops[i]["cost"] and prio[k] - prio[i] > ops[k]["cost"]:
-                    i, t0 = k, rt[k]
-            if best is None or t0 < best[0]:
-                best = (t0, i)
-        t0, i = best
-        ready[ops[i]["eng"]].remove(i)
-        start[i] = t0
-        free[ops[i]["eng"]] = t0 + ops[i]["cost"]
-        order.append(i)
-        for k in succ[i]:
-            rt[k] = max(rt[k], t0 + ops[i]["cost"] + ops[i]["lat"] + WAKE)
-            left[k] -= 1
-            if left[k] == 0:
-                ready[ops[k]["eng"]].append(k)
-    return order, start
+def queues(ops, code):
+    out, k = [], 0
+    for o in ops:
+        names = sorted(o["alts"])
+        pick = 0
+        if len(names) > 1:
+            pick = int(code[k // 3], 36) // 3 ** (k % 3) % 3 if code else 0
+            k += 1
+        out.append(names[pick])
+    return out
 
 
 def plan(ops):
     n = len(ops)
     deps = hazards(ops)
-    order, start = arrange(ops, deps, JIT)
+    eng = queues(ops, QUEUES)
+    order = [int(ORDER[2 * k:2 * k + 2], 36) for k in range(n)] if ORDER else list(range(n))
     count = {e: 0 for e in "vapt"}
     mark, clock, known = [None] * n, [None] * n, {e: {} for e in "vapts"}
     waits = [{} for _ in ops]
     pos = {i: k for k, i in enumerate(order)}
     for i in order:
         o = ops[i]
-        kn = known[o["eng"]]
+        kn = known[eng[i]]
         for j in sorted(deps[i], key=lambda k: -pos[k]):
+            assert pos[j] < pos[i]
             if mark[j] and kn.get(mark[j][0], 0) < mark[j][1]:
                 waits[i][mark[j][0]] = mark[j][1]
                 for s2, v2 in clock[j].items():
                     kn[s2] = max(kn.get(s2, 0), v2)
         if o["sem"] is None:
-            count[o["eng"]] += 1
-            mark[i] = ("c" + o["eng"], count[o["eng"]])
+            count[eng[i]] += 1
+            mark[i] = ("c" + eng[i], count[eng[i]])
         elif o["sem"] != "-":
             mark[i] = (o["sem"], 16)
         clock[i] = dict(kn)
         if mark[i]:
             clock[i][mark[i][0]] = mark[i][1]
-    return {"order": order, "waits": waits, "mark": mark, "count": count, "start": start, "deps": deps}
+    return {"order": order, "eng": eng, "waits": waits, "mark": mark, "count": count}
 
 
 CACHE = {}
@@ -486,26 +526,26 @@ def rank_program(g, core, T, topo):
         CACHE["ops"] = build()
         CACHE["plan"] = plan(CACHE["ops"])
     ops, pl = CACHE["ops"], CACHE["plan"]
-    far = min(len(topo.engines(core, T.cores[rank ^ s])) for s in STEP)
-    ctx = []
+    ctx, width = [], []
     for s in STEP:
         dst = T.cores[rank ^ s]
         rid, pid, _ = topo.addr(dst)
-        ctx.append((rid, pid, sum(1 << e for e in topo.engines(core, dst)[:far])))
+        ctx.append((rid, pid, topo.mask(core, dst)))
+        width.append(len(topo.engines(core, dst)))
     queue = {"v": g.vector, "a": g.scalar, "p": g, "t": g.tensor, "s": g.sync}
     landed = set()
     for i in pl["order"]:
-        o = ops[i]
-        q = queue[o["eng"]]
+        o, e = ops[i], pl["eng"][i]
+        q = queue[e]
         for s, val in pl["waits"][i].items():
             q.wait_ge(T.sem[s], val)
         if o["extra"] and o["extra"] not in landed:
             landed.add(o["extra"])
-            q.wait_ge(T.sem[o["extra"]], 2 * far)
-        ins = o["fn"](g, T, ctx)
+            q.wait_ge(T.sem[o["extra"]], 2 * width[o["part"][0]])
+        ins = o["alts"][e][3](g, T, ctx)
         if pl["mark"][i]:
             ins.then_inc(T.sem[pl["mark"][i][0]], 1 if o["sem"] is None else 16)
-    g.wait_ge(T.sem.sent, 12 * far)
+    g.wait_ge(T.sem.sent, 4 * sum(width))
     for e in "vapt":
         g.sync.wait_ge(T.sem["c" + e], pl["count"][e])
     for name in DMAS:

from concourse.mybir import dt, AluOpType, ActivationFunctionType

A = AluOpType
AF = ActivationFunctionType
F32, BF, I32, U16, Q8, U8 = "float32", "bfloat16", "int32", "uint16", "float8_e4m3fn_x4", "uint8"
SIZE = {F32: 4, BF: 2, I32: 4, U16: 2, Q8: 4, U8: 1}
STEP = [1, 2, 4]
BIGC = 1.0e29
KP, KS = 512.0, 4096.0
OPT = {"pieces": 2, "pre": 1, "fm": 2, "l4": 1, "two": 1, "xg": 1}
SCRATCH, PLACE = {}, {}


def layout():
    n = 256 // OPT["pieces"]
    rw = n + 16 + n * OPT["two"]
    SCRATCH.clear()
    PLACE.clear()
    for ty, pool, names in [
        (I32, "", "fni16 pI8 rI16 dI80 vb256 tb_%d" % (2 * rw)),
        (U16, "", "cl8 fl80 ul64 il16 ho_2 lp_16 rk_16 sl_16"),
        (BF, "", "ut512 vt512 et516 pz640 x_640 xw_1056 xg_512 z_512 zz_512 y_640 ph_128 pn_128 nf_128 sh_128"),
        (BF, "kb", "eh32 sg32 tw32 cc256 cn256 lc256 smb96 cs256 da128 db128 tn272 tc272 ci128"),
        (BF, "hb", "rf256 ra256 rb256 rc256 rd256 ex256 ma256 mc256 sn256 sx256 hw_272 rs256 nc256 cf256 po768"),
        (BF, "ub", "uo_%d" % (3 * rw)),
        (BF, "zb", "pp%d pr_%d ta_%d tu_%d" % (rw, 3 * rw, 2 * rw, rw)),
        (F32, "", "col48 fof256 yo256 mb_136 sa_32 iw_288"),
        (F32, "kf", "kx16 kk16 sm160 cm128 jb128 wb256 so256 cd768 sr256 pf_16"),
        (F32, "zf", "wa%d sp%d ck_%d sq_%d tg_%d" % (rw, rw, 5 * rw, rw, 2 * rw)),
        (Q8, "", "wq512 uq128 ur128 vq128 eq512 qx256 qz_128 pqa_160 pqb_160 pqc_160"),
        (U8, "", "wp512 us128 uu128 vp128 ep512 ox256 sz_128 ppa_160 ppb_160 ppc_160"),
    ]:
        at = 0
        for e in names.split():
            k = len(e.rstrip("0123456789"))
            for s in (["0", "1"] if e[k - 1] == "_" else [""]):
                if pool:
                    PLACE[e[:k] + s] = (pool, at)
                    at += int(e[k:])
                else:
                    SCRATCH[e[:k] + s] = ("sbuf", [128, int(e[k:])], ty)
        if pool:
            SCRATCH[pool] = ("sbuf", [128, at], ty)
    SCRATCH["ps"] = ("psum", [128, 4096], F32)


layout()
DMAS = ["fn", "x0", "x1", "u", "v", "wc", "ws", "fo", "y0", "y1", "oc0", "oc1", "os0", "os1", "os2", "os3"]
SEMAPHORES = ["cv", "ca", "cp", "ct", "sent"] + ["d_" + _n for _n in DMAS] + ["arr%d_%d" % (_r, _h) for _r in range(3) for _h in range(2)]

CYC = 0.00104
QUEUES = "dd493da0000009c3030900c100000000204009mc000093a39911a3900016100da0900000mc90900da13"
ORDER = "0001020304050607112e152n0809280l130j0z0g2o0m0o0n160d0i1v0y314s1w0r0p0h322z0q0f144t0e0t0s0b300k332p0x4u2u34531z1j173n354v1c3c0v1d364w266j0w1b6m4x0u372h5e1x2310381i124y0c6k392r0a6n4z3d2q6l2t503a832m1t3e1s3b272v2i5154183i3f862a2w551q59522x1u3g56192l218c243h2d298a6s2f57221n8d1o3j1k3k6t1r1e583l3m2j2s1y3o3p1p1g5b842k205a6o8b3q6q2b5d5c8e3r6u1m5g5f6p3s8f2c6v1a255h2g1l3t2y855i6w4f1h3u446r5j4o884g3v455k8g433w5l5v5w663x5m4p4h1f67893y5n465o3z47684i5x405p48695y5q4j4987416a5r425z4k4a6b5s604l6c4b5t4m616d4c4n6f4q624e6e6x4d63726y758h646z5u7865737b766g4r798s7c8m708i7e778j6h8p7g8n7a7h8v8q7i7d7f747k8r7l717m7j8w7n8t8x6i7o8y7t7p8o8k8u908l91958z92947q9396979c7u7v9d98997s7x9b7z7r7w7y9a9f8180829e9h9g9s9u9j9i9l9t9k9n9m9v9w9xbeb7ba9y9zbcbgbb9o9qa0bh9p9rb8a1bda2a4a6bib9a3a5a9bja7bfacbkaaafblada8bqbmagbtbnabbwaibrbzambuaealahbxajc0akbyaqapbvc1c2anaoc5boc6arbpc9c4bscaavc3asawc8c7auaxatcbccb0cgazcdcfb4ceb1b3ayb5chb2clcib6cuckcjcpcocmcwcncrcqcvd0cxcscyd1czedeeeid2emctd3ekegd4enejd5eodcd6efd8epd7dfeheqdddieresdldgeydjf1etdmf4ezeldof7f2dpewf5drdef8dkdqdhd9dndsdtdafadvf9dufef0dwdxf6fdeufifcevfhf3dbfbdydze0fge1ffexfjg9fnfkfpe5foe7fle2fme4e3e6e9e8ebfteafrecfsfqfwfvfxfufzfyg3g0g1g4g5gagdg8gcgbg2g6g7"


def V(name, a, b, s=1):
    name, at = PLACE.get(name, (name, 0))
    return (name, at + a, at + b, s)


def cnt(v):
    return len(range(v[1], v[2], v[3]))


def dty(v):
    return SCRATCH[v[0]][2]


def ap(T, v):
    if v[3] == 1:
        return T[v[0]][:, v[1]:v[2]]
    return T[v[0]][:, v[1]::v[3]] if v[2] < 0 else T[v[0]][:, v[1]:v[2]:v[3]]


def rev(v):
    return (v[0], v[2] - 1, v[1] - 1, -1)


def build():
    ops, part = [], [(-1, -1)]
    n = 256 // OPT["pieces"]
    RW, SENT = n + 16 + n * OPT["two"], n + 4
    WL = SENT + n * OPT["two"]

    def add(alts, reads, writes, sem=None, extra=None, after=()):
        ops.append({"alts": alts, "r": [x for x in reads if isinstance(x, tuple)], "w": writes, "sem": sem, "extra": extra,
                    "after": list(after), "part": part[0]})
        return len(ops) - 1

    def sc(T, s):
        return ap(T, s) if isinstance(s, tuple) else s

    def src(T, v, ind):
        return ap(T, v).indirect(ap(T, ind)) if ind else ap(T, v)

    def vcost(out, ins, ind, two=False):
        half = all(SIZE[dty(x)] == 2 for x in [out] + ins)
        return ("g", 0.05, cnt(out)) if ind else ("c", max(64, cnt(out) * (2 if two else 0.5 if half else 1)) * CYC, 0)

    def vec(out, ins, more, ind, fn, two=False):
        return add({"v": vcost(out, ins, ind, two) + (fn,)}, ins + more + [ind], [out])

    def cp(out, in_, ind=None):
        return vec(out, [in_], [], ind, lambda g, T, c: g.vector.tensor_copy(ap(T, out), src(T, in_, ind)))

    def scat(win, ind, in_):
        return add({"v": ("s", 0.05, cnt(in_), lambda g, T, c: g.vector.tensor_copy(ap(T, win).indirect(ap(T, ind)), ap(T, in_)))},
                   [in_, ind], [win])

    def tt(out, a, b, op, ind=None):
        return vec(out, [a, b], [], ind, lambda g, T, c: g.vector.tensor_tensor(ap(T, out), src(T, a, ind), ap(T, b), op), a[0] != "ps")

    def tsfn(out, a, s1, op0, s2, op1, ind):
        def fn(g, T, c):
            if op1 is None:
                return g.vector.tensor_scalar(ap(T, out), src(T, a, ind), sc(T, s1), None, op0)
            return g.vector.tensor_scalar(ap(T, out), src(T, a, ind), sc(T, s1), sc(T, s2), op0, op1)
        return fn

    def ts(out, a, s1, op0, s2=None, op1=None, ind=None):
        return vec(out, [a], [s1, s2], ind, tsfn(out, a, s1, op0, s2, op1, ind))

    def scan(out, d0, d1, op0, op1, init=0.0):
        return vec(out, [d0, d1], [], None, lambda g, T, c: g.vector.tensor_tensor_scan(ap(T, out), ap(T, d0), ap(T, d1), init, op0, op1))

    def iotafn(out, pat, base, cm):
        def fn(g, T, c):
            if dty(out) == I32:
                return g.iota(ap(T, out), pat, base, cm)
            return g.iota(ap(T, out), pat, base, cm, allow_small_or_imprecise_dtypes=True)
        return ("c", 0.16 + 2 * cnt(out) * CYC, 0, fn)

    def iota(out, pat, base, cm=0):
        return add({"p": iotafn(out, pat, base, cm)}, [], [out])

    def fill(out, val):
        return add({"v": vcost(out, [], None) + (lambda g, T, c: g.vector.memset(ap(T, out), float(val)),),
                    "p": iotafn(out, [[0, cnt(out)]], val, 0)}, [], [out])

    def selfn(out, in_, pat, op, val, base, cm):
        return ("c", 0.21 + 2 * cnt(out) * CYC, 0, lambda g, T, c: g.affine_select(ap(T, out), ap(T, in_), pat, op, val, base, cm))

    def select(out, in_, pat, op, val, base=0, cm=0):
        return add({"p": selfn(out, in_, pat, op, val, base, cm)}, [in_], [out])

    def lin(out, in_, scale=None, bias=None, ind=None):
        def afn(g, T, c):
            s = 1.0 if scale is None else sc(T, scale)
            if bias is None:
                return g.scalar.activation(ap(T, out), src(T, in_, ind), AF.Copy, scale=s)
            return g.scalar.activation(ap(T, out), src(T, in_, ind), AF.Identity, bias=sc(T, bias), scale=s)
        alts = {"a": (("g", 0.065, cnt(out)) if ind else ("c", max(64, cnt(out)) * CYC, 0)) + (afn,)}
        if scale is None and bias is None:
            vfn = lambda g, T, c: g.vector.tensor_copy(ap(T, out), src(T, in_, ind))
            if not ind and in_[0] != "ps":
                alts["p"] = selfn(out, in_, [[0, cnt(out)]], A.is_ge, 0.0, 0, 0)
        elif bias is None:
            vfn = tsfn(out, in_, scale, A.mult, None, None, ind)
        elif scale is None:
            vfn = tsfn(out, in_, bias, A.add, None, None, ind)
        else:
            vfn = tsfn(out, in_, scale, A.mult, bias, A.add, ind)
        alts["v"] = vcost(out, [in_], ind) + (vfn,)
        return add(alts, [in_, scale, bias, ind], [out])

    def quant(q, s, in_):
        return add({"v": ("q", 0.012 + 0.00022 * cnt(in_), 0, lambda g, T, c: g.vector.quantize_mx(ap(T, q), ap(T, s), ap(T, in_)))},
                   [in_], [q, s])

    def mm(bank, lq, lsc, rq, rs, extra=None, after=()):
        out = V("ps", 512 * bank, 512 * bank + cnt(rq))
        return add({"t": ("t", (cnt(rq) + 16) * 0.00125, 0,
                          lambda g, T, c: g.tensor.matmul_mx(ap(T, out), ap(T, lq), ap(T, lsc), ap(T, rq), ap(T, rs), True, True))},
                   [lq, lsc, rq, rs], [out], extra=extra, after=after)

    def dma(name, reads, writes, fo, fi):
        return add({"s": ("d", 0.06, name, lambda g, T, c: g.sync.dma_start(fo(T), fi(T))),
                    "a": ("d", 0.06, name, lambda g, T, c: g.scalar.dma_start(fo(T), fi(T)))}, reads, writes, sem="d_" + name)

    def C(k, m=1):
        return V("col", k, k + m)

    def W(name, k=0, m=128, stride=128):
        return V(name, stride * k, stride * k + m)

    dma("fn", [], [W("fni", 0, 16)], lambda T: T.fni[:], lambda T: T.fn[:])
    dma("u", [], [W("ut", 0, 512)], lambda T: T.ut[:], lambda T: T.u[:])
    for h in range(2):
        dma("x%d" % h, [], [V("x_%d" % h, 128, 640)], lambda T, h=h: T["x_%d" % h][:, 128:640], lambda T, h=h: T.x[:, 512 * h:512 * h + 512])
    dma("wc", [], [W("wq", 0, 512)], lambda T: T.wq[:].bitcast(dt.uint8), lambda T: T.wc[:])
    dma("ws", [], [W("wp", 0, 512)], lambda T: T.wp[:], lambda T: T.ws[:])
    dma("v", [], [W("vt", 0, 512)], lambda T: T.vt[:], lambda T: T.v[:])

    B0, B1, B2, B3, R3, BLK, R = range(7)
    K0, F0, G2, H2, Q2 = 8, 12, 16, 18, 20
    S16, R16, DA, DB, UNP, SCL, UNS, H0, RS, T0, R128, HC = range(22, 34)
    iota(V("dI", 0, 32), [[1, 32]], 128, -1)
    iota(V("pI", 0, 1), [[0, 1]], 0, 1)
    iota(V("cc", 0, n), [[1, n]], 1)
    iota(V("eh", 0, 32), [[1, 32]], 0)
    iota(V("sg", 0, 32), [[2, 2], [0, 16]], -1)
    iota(W("kx", 0, 16), [[16, 16]], 0)
    for k, (s, m) in enumerate([(0, 1), (1, 1), (2, 1), (3, 1), (0, 3), (1, 3), (0, 15)]):
        ts(V("rI", k, k + 1), V("pI", 0, 1), s, A.logical_shift_right, m, A.bitwise_and)
    cp(C(B0, 7), V("rI", 0, 7))
    ts(V("dI", 32, 64), V("dI", 0, 32), 15, A.bitwise_and)
    ts(V("smb", 0, 32), V("dI", 32, 64), 0.0, A.not_equal)
    ts(V("smb", 32, 64), V("dI", 32, 64), 1.0, A.is_equal, 1024.0, A.mult)
    ts(V("smb", 64, 96), V("dI", 32, 64), 0.0, A.is_equal)
    ts(C(S16), V("smb", 79, 80), 2.0 ** -10, A.max)
    for k in range(0, 128, 32):
        tt(V("cs", k, k + 32), V("smb", 0, 32), V("smb", 32, 64), A.max)
    if n == 256:
        lin(V("cs", 128, 256), V("cs", 0, 128))
    lin(C(R16), C(R), bias=16.0)
    lin(C(DA), C(R), bias=-129.0)
    lin(C(DB), C(R), scale=-1.0, bias=113.0)
    tt(V("tw", 0, 32), V("smb", 64, 96), V("sg", 0, 32), A.mult)
    for h in range(n // 128):
        lin(W("cn", h), W("cc"), scale=-1.0, bias=257.0)
    lc = V("cc", 0, n)
    if n == 256:
        lc = V("lc", 0, n)
        lin(lc, V("cn", 0, n), scale=-1.0, bias=257.0)
    fill(W("da"), -1024)
    lin(V("da", 0, 128, 32), V("cc", 0, 128, 32), bias=C(DA))
    fill(W("db"), 1024)
    lin(V("db", 0, 128, 32), V("cc", 0, 128, 32), scale=-1.0, bias=C(DB))
    for name, val in (("tn", 1), ("tc", -n)):
        fill(V(name, 0, 129), 0)
        fill(V(name, 129, 257), val)
    lin(C(K0, 4), C(B0, 4), scale=KP)
    lin(C(F0, 4), C(B0, 4), scale=1.0 / KP - 1.0, bias=1.0)
    ts(C(T0), C(F0), C(F0 + 1), A.mult, C(F0 + 2), A.mult)
    lin(C(UNP), C(T0), scale=C(F0 + 3))
    lin(C(G2, 2), C(B2, 2), scale=KS)
    lin(C(H2, 2), C(B2, 2), scale=KS - 1.0, bias=1.0)
    lin(C(Q2, 2), C(B2, 2), scale=1.0 / KS - 1.0, bias=1.0)
    lin(C(SCL), C(H2), scale=C(H2 + 1))
    lin(C(UNS), C(Q2), scale=C(Q2 + 1))
    lin(C(RS), C(R), scale=C(SCL))
    lin(W("kk", 0, 16), W("kx", 0, 16), scale=C(SCL), bias=C(RS))
    lin(V("pp", 0, n), lc, scale=C(K0))
    lin(C(R128), C(R3), bias=124.0)
    lin(V("so", 0, n), lc, scale=4.0, bias=C(R128))
    lin(V("sp", 0, n), V("so", 0, n), scale=C(G2))
    for name, val in (("ub", SENT), ("zb", 0), ("zf", 0)):
        for k in sorted({SENT, WL}):
            fill(V(name, k - 1, SCRATCH[name][1][1], RW), val)
    ts(V("sm", 0, 32), V("eh", 0, 32), C(R), A.is_lt)
    ts(V("sm", 32, 64), V("eh", 0, 32), C(R16), A.is_lt, 2048.0, A.mult)
    tt(V("sm", 64, 96), V("sm", 0, 32), V("sm", 32, 64), A.add)
    lin(V("sm", 128, 144), V("smb", 64, 80))
    lin(V("sm", 144, 160), V("smb", 80, 96), scale=2048.0)
    for b in range(4):
        lin(W("jb", b, 32, 32), V("sm", 128, 160), scale=160.0 + 32.0 * b)
        tt(W("wa", b, 32, 32), W("jb", b, 32, 32), V("sm", 64, 96), A.add)
    for out in [W("wb")] + ([W("wa", 1), W("wb", 1)] if n == 256 else []):
        lin(out, W("wa"))
    iota(W("nf_0"), [[1, 4], [0, 32]], 0)
    ts(W("ci"), W("nf_0"), C(BLK), A.is_equal)
    fill(W("cm"), 0)
    lin(V("cm", 0, 128, 32), V("ci", 0, 128, 32), scale=-BIGC)
    lin(V("cm", 31, 128, 32), V("ci", 0, 128, 32), scale=BIGC)
    lin(C(H0), C(BLK), scale=32.0, bias=32.0)
    lin(C(HC), C(B0), scale=float(RW), bias=C(H0))
    if n == 256:
        lin(C(HC + 1), C(HC), bias=128.0)
    for h in range(2):
        fill(V("mb_%d" % h, 0, 1), 0)
        fill(V("y_%d" % h, 0, 128), 0)
        fill(V("hw_%d" % h, 128, 129), SENT)
        fill(V("pf_%d" % h, 8, 16), 0)
        iota(V("iw_%d" % h, 32, 160), [[1, 128]], 128 * h)
    fill(V("pz", 128, 512), 0)
    fill(W("et", 0, 516), 0)
    select(W("et", 0, 516), W("et", 0, 516), [[1, 516]], A.not_equal, 0.5, -3, -4)
    for b in range(4):
        quant(W("eq", b), W("ep", b), V("et", 3 - b, 515 - b))
    quant(W("uq"), W("us"), W("ut", 0, 512))
    cl = V("cl", 0, 8)
    cp(cl, V("kx", 0, 8))
    add({"v": ("g", 0.05, 128, lambda g, T, c: g.vector.tensor_copy(
        T.ur[:, 0:128].bitcast(dt.uint32), T.uq[:, 0:128].bitcast(dt.uint32).indirect(T.cl[:, 0:8])))}, [W("uq"), cl], [W("ur")])
    add({"a": ("g", 0.065, 128, lambda g, T, c: g.scalar.activation(T.uu[:, 0:128], T.us[:, 0:128].indirect(T.cl[:, 0:8]), AF.Copy))},
        [W("us"), cl], [W("uu")])
    quant(W("vq"), W("vp"), W("vt", 0, 512))

    ts(V("dI", 64, 80), W("fni", 0, 16), 31, A.bitwise_and)
    cp(W("fl", 4, 16, 16), V("dI", 64, 80))
    for pc in range(OPT["pieces"]):
        halves = [pc] if n == 128 else [0, 1]
        part[0] = (-1, pc)

        def H(name, k=0):
            return V(name, 256 * k + n * pc, 256 * k + n * pc + n)

        def G(name, k=0, m=n):
            return W("%s_%d" % (name, pc), k, m, RW)

        def L(name, k):
            return V(name, 16 * k + n // 16 * pc, 16 * k + n // 16 * (pc + 1))

        def extract(lst, row):
            scan(H("ex"), V("cs", 0, n), row, A.mult, A.max)
            ts(lst, V("ex", n * pc + 15, n * pc + n, 16), C(S16), A.mult, -1.0, A.add)

        FL, UL = [L("fl", k) for k in range(5)], [L("ul", k) for k in range(4)]
        ts(FL[0], L("fni", 0), -1.0 * n * pc, A.add)
        rows = [V("cc", 0, n), H("rf"), H("ra"), H("rb"), H("rc"), H("ra")]
        if OPT["fm"] == 2:
            for k in range(4):
                lin(rows[k + 1], rows[k], ind=FL[max(k - 1, 0)])
                if k:
                    extract(FL[k], rows[k + 1])
            pulls = [2, 2, 3, 3, 3] if OPT["pre"] else [3, 3, 3, 3]
        else:
            for k in range(5):
                lin(rows[k + 1], rows[k], ind=FL[k // 3])
                if k in (2, 4):
                    extract(FL[k // 2], rows[k + 1])
            pulls = [0, 1, 1, 1, 1, 2, 2]
        tt(H("ma"), V("tw", 0, 32), V("cn", 0, n), A.mult, ind=FL[4])
        m0, m1 = "ma", "mc"
        for lst in pulls:
            lin(H(m1), H(m0), ind=FL[lst])
            m0, m1 = m1, m0
        select(H("rs"), H("rf"), [[0, n // 32], [1, 32]], A.not_equal, float(SENT + n))
        for h in halves:
            il, hw = W("il", h, 8, 8), "hw_%d" % h
            scan(W("sn", h), W("da"), W(m0, h), A.max, A.min, -1024.0)
            scan(W("sx", h), W("db"), W(m0, h), A.min, A.max, 1024.0)
            ts(V("il", 8 * h, 8 * h + 8, 2), V("sn", 128 * h + 31, 128 * h + 128, 32), 257.0, A.add)
            ts(V("il", 8 * h + 1, 8 * h + 8, 2), V("sx", 128 * h + 31, 128 * h + 128, 32), -1.0, A.mult, 257.0, A.add)
            lin(V(hw, 129, 257), W("rf", h))
            lin(W("nc", h), V("tn", 0, 257), ind=il)
            tt(W("cf", h), V("tc", 0, 257), W("rs", h), A.add, ind=il)
            scan(rev(W(hw)), rev(W("nc", h)), rev(W("cf", h)), A.mult, A.max, float(SENT))
            if OPT["two"]:
                lin(W("uo_%d" % pc, h - halves[0]), V(hw, 0, 257), ind=il)
            else:
                ts(W("uo_%d" % pc, h - halves[0]), V(hw, 0, 257), float(SENT), A.min, ind=il)
        extract(UL[0], G("uo"))
        for k in range(3):
            out = G("uo", k + 1) if k < 2 else H("rd")
            lin(out, G("uo", k, WL), ind=UL[k])
            extract(UL[k + 1], out)
        for h in halves:
            ts(V("pf_%d" % h, 0, 8), W("ul", h, 8, 8), 32.0 - 128.0 * (h - halves[0]), A.add, 159.0, A.min)
        for k in range(4):
            if k == 3 and OPT["l4"]:
                lin(G("ck", 4), G("ck", 2, WL), ind=UL[2])
                tt(G("ck", 3), G("ck", 4, WL), G("ck", 2), A.add, ind=UL[2])
                continue
            if k:
                lin(H("cd", k - 1), G("ck", k - 1))
            tt(G("ck", k), G("ck", k - 1, WL) if k else V("wa", 0, WL), H("cd", k - 1) if k else V("wb", 0, n), A.add, ind=UL[k])
        lin(G("ck", 4), G("ck", 3, WL), ind=UL[3])
        tt(H("vb"), G("ck", 4, WL), G("ck", 3), A.add, ind=UL[3])
        for h in halves:
            at = 128 * (h - halves[0])
            ts(V("tb_%d" % pc, at, at + 128), W("vb", h), 2047, A.bitwise_and)
            ts(V("tb_%d" % pc, RW + at, RW + at + 128), W("vb", h), 11, A.logical_shift_right)
        for k in range(4):
            if k == 2 and OPT["l4"]:
                lin(G("pr", 1), H("po", 1), scale=C(K0 + 2))
                tt(G("tu"), G("pr", 1, WL), H("po", 1), A.max, ind=UL[2])
                lin(G("pr", 2), G("tu", 0, WL), scale=C(K0 + 3), ind=UL[2])
                tt(G("ta"), G("pr", 2, WL), G("tu"), A.max, ind=UL[2])
                break
            if k:
                lin(G("pr", k - 1), H("po", k - 1), scale=C(K0 + k))
            tt(H("po", k) if k < 3 else G("ta"), G("pr", k - 1, WL) if k else V("pp", 0, WL), H("po", k - 1) if k else lc, A.max, ind=UL[k])
        lin(G("tu"), G("ta", 0, WL), ind=UL[3])
        lin(G("ta", 1), G("tu", 0, WL), ind=UL[3])
        tt(H("sr"), V("sp", 0, WL), V("so", 0, n), A.max, ind=UL[0])
        lin(G("sq"), H("sr"), scale=C(G2 + 1))
        tt(G("tg"), G("sq", 0, WL), H("sr"), A.max, ind=UL[1])
        lin(G("tg", 1), G("tg", 0, WL), ind=UL[2])

    for t in range(4):
        for h in range(2):
            def N(s, a, b, st=1):
                return V("%s_%d" % (s, h), a, b, st)

            def PS(b, m=128):
                return W("ps", 4 * h + b, m, 512)

            def TB(name):
                return V("%s_%d" % (name, h if n == 128 else 0), 0, RW + n)
            part[0] = (t, h)
            qx, sx = W("qx", h), W("ox", h)
            quant(qx, sx, N("x", 128, 640))
            if t == 3:
                mm(4 * h, W("vq"), W("vp"), qx, sx)
                yo = W("yo", h)
                lin(yo, PS(0))
                dma("y%d" % h, [yo], [], lambda T, h=h: T.y[:, 128 * h:128 * h + 128], lambda T, yo=yo: ap(T, yo))
                dma("oc%d" % h, [qx], [], lambda T, h=h: T.oc[:, 512 * h:512 * h + 512], lambda T, qx=qx: ap(T, qx).bitcast(dt.uint8))
                continue
            for b in range(4):
                lin(N("xw", 32 + 256 * b, 160 + 256 * b), N("x", 128 + b, 640, 4), scale=0.5)
                if OPT["xg"]:
                    lin(N("xg", 128 * b, 128 * b + 128), N("xw", 32 + 256 * b, 160 + 256 * b))
                else:
                    lin(N("xg", 128 * b, 128 * b + 128), N("x", 128 + b, 640, 4), scale=0.5)
            mm(4 * h, W("ur"), W("uu"), qx, sx)
            scan(N("mb", 1, 129), W("cm"), PS(0), A.add, A.max)
            tt(N("nf", 0, 128), PS(0), N("mb", 0, 128), A.is_le)
            scan(N("sh", 0, 128), N("nf", 0, 128), W("ci"), A.mult, A.add)
            ho = N("ho", 0, 1)
            ts(ho, N("sh", 127, 128), -1.0, A.mult, C(HC + (h if n == 256 else 0)), A.add)
            ts(N("lp", 0, 16), TB("ta"), C(UNP), A.mult, -1.0, A.add, ind=ho)
            tt(N("sa", 0, 16), TB("tb"), N("pf", 0, 16), A.max, ind=ho)
            cp(N("rk", 0, 8), N("sa", 0, 8))
            tt(N("sa", 16, 32), TB("tg"), W("kk", 0, 16), A.max, ind=ho)
            ts(N("sl", 0, 8), N("sa", 16, 24), C(UNS), A.mult)
            if t == 2:
                lin(N("iw", 160, 288), N("iw", 32, 160), ind=N("lp", 0, 8))
                lin(W("fof", h), N("iw", 0, 288), ind=N("rk", 0, 8))
            for b in range(4):
                lin(N("xw", 160 + 256 * b, 288 + 256 * b), N("xw", 32 + 256 * b, 160 + 256 * b), ind=N("lp", 0, 8))
                tt(N("z", b, 512, 4), N("xw", 256 * b, 256 * b + 288), N("xg", 128 * b, 128 * b + 128), A.add, ind=N("rk", 0, 8))
                lin(N("zz", 128 * b, 128 * b + 128), N("z", b, 512, 4), scale=32.0)
            quant(N("qz", 0, 128), N("sz", 0, 128), N("z", 0, 512))
            for b in range(4):
                mm(4 * h + b, W("wq", b), W("wp", b), N("qz", 0, 128), N("sz", 0, 128))
            for b in range(4):
                tt(N("y", 128 + b, 640, 4), PS(b), N("zz", 128 * b, 128 * b + 128), A.add)
            pt = V("pz", 512 * h, 512 * h + 128)
            lin(pt, N("y", 0, 640), scale=2.0 ** -5, ind=N("sl", 0, 8))
            pq, pp, arr = "pq%s_%d" % ("abc"[t], h), "pp%s_%d" % ("abc"[t], h), "arr%d_%d" % (t, h)
            quant(V(pq, 32, 160), V(pp, 32, 160), V("pz", 128 * h, 128 * h + 512))
            a = 32 + 96 * h

            def send(g, T, c, name, codes, t=t, arr=arr, a=a):
                rid, pid, mask = c[t]
                o, i = T[name][:, 0:32], T[name][:, a:a + 32]
                if codes:
                    o, i = o.bitcast(dt.uint8), i.bitcast(dt.uint8)
                g.remote_dma(o, i, T.sem[arr], T.sem.sent, pid, rid, mask)
            s1 = add({"p": ("r", 0.2, 0, lambda g, T, c, f=send, m=pq: f(g, T, c, m, True))}, [V(pq, a, a + 32)], [], sem="-")
            s2 = add({"p": ("r", 0.2, 0, lambda g, T, c, f=send, m=pp: f(g, T, c, m, False))}, [V(pp, a, a + 32)], [], sem="-")
            for q in (0, 256):
                lin(N("x", 128 + q, 384 + q), N("y", 128 + q, 384 + q), scale=2.0 ** -5)
            lin(N("ph", 0, 128), pt, scale=0.5)
            for b in range(4):
                mm(4 * h + b, W("eq", b), W("ep", b), V(pq, 0, 128), V(pp, 0, 128), extra=arr, after=(s1, s2))
            for b in range(4):
                tt(N("pn", b, 128, 4), PS(b, 32), N("ph", b, 128, 4), A.add)
            scat(N("x", 0, 640), N("sl", 0, 8), N("pn", 0, 128))
    dma("fo", [W("fof", 0, 256)], [], lambda T: T.fo[:], lambda T: T.fof[0:128:16, :])
    for k in range(4):
        dma("os%d" % k, [W("ox", 0, 256)], [], lambda T, k=k: T.osc[4 * k:4 * k + 4, :], lambda T, k=k: T.ox[32 * k:32 * k + 4, :])
    return ops


def cells(v):
    return set([v[1] // 512]) if v[0] == "ps" else set(range(v[1], v[2], v[3]))


def hazards(ops):
    hist = {}
    deps = [set(o["after"]) for o in ops]
    for i, o in enumerate(ops):
        acc = [(v, v[0] == "ps") for v in o["r"]] + [(v, True) for v in o["w"]]
        for v, wr in acc:
            cs = cells(v)
            for j, cj, wj in hist.get(v[0], []):
                if (wr or wj) and not cs.isdisjoint(cj):
                    deps[i].add(j)
        for v, wr in acc:
            hist.setdefault(v[0], []).append((i, cells(v), wr))
    return deps


def queues(ops, code):
    out, k = [], 0
    for o in ops:
        names = sorted(o["alts"])
        pick = 0
        if len(names) > 1:
            pick = int(code[k // 3], 36) // 3 ** (k % 3) % 3 if code else 0
            k += 1
        out.append(names[pick])
    return out


def plan(ops):
    n = len(ops)
    deps = hazards(ops)
    eng = queues(ops, QUEUES)
    order = [int(ORDER[2 * k:2 * k + 2], 36) for k in range(n)] if ORDER else list(range(n))
    count = {e: 0 for e in "vapt"}
    mark, clock, known = [None] * n, [None] * n, {e: {} for e in "vapts"}
    waits = [{} for _ in ops]
    pos = {i: k for k, i in enumerate(order)}
    for i in order:
        o = ops[i]
        kn = known[eng[i]]
        for j in sorted(deps[i], key=lambda k: -pos[k]):
            assert pos[j] < pos[i]
            if mark[j] and kn.get(mark[j][0], 0) < mark[j][1]:
                waits[i][mark[j][0]] = mark[j][1]
                for s2, v2 in clock[j].items():
                    kn[s2] = max(kn.get(s2, 0), v2)
        if o["sem"] is None:
            count[eng[i]] += 1
            mark[i] = ("c" + eng[i], count[eng[i]])
        elif o["sem"] != "-":
            mark[i] = (o["sem"], 16)
        clock[i] = dict(kn)
        if mark[i]:
            clock[i][mark[i][0]] = mark[i][1]
    return {"order": order, "eng": eng, "waits": waits, "mark": mark, "count": count}


CACHE = {}


def rank_program(g, core, T, topo):
    rank = T.rank_of(core)
    if rank is None:
        return
    if not CACHE:
        CACHE["ops"] = build()
        CACHE["plan"] = plan(CACHE["ops"])
    ops, pl = CACHE["ops"], CACHE["plan"]
    ctx, width = [], []
    for s in STEP:
        dst = T.cores[rank ^ s]
        rid, pid, _ = topo.addr(dst)
        ctx.append((rid, pid, topo.mask(core, dst)))
        width.append(len(topo.engines(core, dst)))
    queue = {"v": g.vector, "a": g.scalar, "p": g, "t": g.tensor, "s": g.sync}
    landed = set()
    for i in pl["order"]:
        o, e = ops[i], pl["eng"][i]
        q = queue[e]
        for s, val in pl["waits"][i].items():
            q.wait_ge(T.sem[s], val)
        if o["extra"] and o["extra"] not in landed:
            landed.add(o["extra"])
            q.wait_ge(T.sem[o["extra"]], 2 * width[o["part"][0]])
        ins = o["alts"][e][3](g, T, ctx)
        if pl["mark"][i]:
            ins.then_inc(T.sem[pl["mark"][i][0]], 1 if o["sem"] is None else 16)
    g.wait_ge(T.sem.sent, 4 * sum(width))
    for e in "vapt":
        g.sync.wait_ge(T.sem["c" + e], pl["count"][e])
    for name in DMAS:
        g.sync.wait_ge(T.sem["d_" + name], 16)
